import numpy as np
import ml_dtypes


def mxq(x, axis, fmt="e4m3"):
    dtype, down = {"e4m3": (ml_dtypes.float8_e4m3fn, 7), "e5m2": (ml_dtypes.float8_e5m2, 14)}[fmt]
    v = np.moveaxis(np.asarray(x, np.float32).astype(ml_dtypes.bfloat16).astype(np.float64), axis, -1)
    blocks = v.reshape(v.shape[:-1] + (-1, 32))
    amax = np.abs(blocks).max(-1, keepdims=True)
    byte = np.maximum(np.where(amax > 0, np.frexp(amax)[1] - 1 + 127, 0) - down, 1)
    scale = np.exp2(byte - 127.0)
    codes = (blocks / scale).astype(np.float32).astype(dtype).astype(np.float64)
    return np.moveaxis((codes * scale).reshape(v.shape), -1, axis)


WIDE = False


def mx_kscale(k):
    if not WIDE:
        return np.ones(k)
    levels = np.array([10, -10, 5, -5, 0])
    if k % 512:
        return np.exp2(np.random.permutation(np.resize(levels, k // 32))).repeat(32)
    a = np.empty((k // 512, 16))
    for p in range(k // 512):
        a[p, :8] = np.random.permutation(np.resize(levels, 8))
        for g in range(8):
            far = levels[np.abs(levels - a[p, g]) >= 10]
            a[p, g + 8] = far[np.random.randint(len(far))]
    return np.exp2(a.ravel()).repeat(32)


def f64(x):
    return np.asarray(x).astype(np.float64)


def striped(idx):
    return np.tile(idx.reshape(-1, 16).T, (8, 1)).astype(np.uint16)


def unstriped(offs):
    return offs[:16].T.reshape(-1).astype(np.int64)


def pack_weight(w):
    k, n = w.shape
    w = f64(np.asarray(w, np.float32).astype(ml_dtypes.bfloat16)).reshape(k // 32, 32, n)
    amax = np.abs(w).max(1)
    byte = np.clip(np.where(amax > 0, np.frexp(amax)[1] - 1 + 127 - 7, 1), 1, 254)
    scaled = (w * np.exp2(127.0 - byte)[:, None, :]).reshape(k, n).astype(np.float32)
    words = np.ascontiguousarray(scaled.reshape(k // 512, 128, 4, n).transpose(0, 1, 3, 2)).astype(ml_dtypes.float8_e4m3fn).view(np.uint8)
    return words, np.ascontiguousarray(byte.astype(np.uint8).reshape(k // 512, 16, n))


def unpack_weight(words, scales):
    g, p, n, _ = words.shape
    vals = np.ascontiguousarray(words).view(ml_dtypes.float8_e4m3fn).astype(np.float64) * np.repeat(np.exp2(scales.astype(np.float64) - 127.0), 8, axis=1)[..., None]
    return vals.transpose(0, 1, 3, 2).reshape(g * 512, n)


K, T, S, H, D, V, W, U = 1024, 1024, 512, 512, 8, 128, 2048, 1024
P = 2 ** 7


def setup_inputs():
    n = np.random.standard_normal
    s = mx_kscale(K)[:, None]
    u = mx_kscale(H)
    packed_xT = pack_weight(n((K, T)) * s)
    packed_eT = pack_weight(n((H, W)) / np.sqrt(H) / u[:, None])
    return {
        "x_words": packed_xT[0],
        "x_scales": packed_xT[1],
        "w1": (n((K, H)) / np.sqrt(K) / s * u).astype(np.float32),
        "e_words": packed_eT[0],
        "e_scales": packed_eT[1],
        "half": (np.tile(np.random.uniform(0.2, 1.0, W), (P, 1))).astype(np.float32),
        "prior": (np.tile(0.5 * n(V), (P, 1))).astype(np.float32),
        "offs": striped(np.random.permutation(T)[:S]),
        "pro": striped(np.random.permutation(W)[:U]),
    }


def reference(x_words, x_scales, w1, e_words, e_scales, half, prior, offs, pro):
    xq = unpack_weight(x_words, x_scales)[:, unstriped(offs)]
    h = mxq(f64(w1), 0, "e4m3").T @ xq
    e_pro = unpack_weight(e_words, e_scales)[:, unstriped(pro)]
    y = mxq(h, 0, "e4m3").T @ e_pro
    ee = np.exp(y - (f64(half)[:1][:, unstriped(pro)]))
    return np.log(ee.reshape(len(ee), -1, D).sum(axis=2)) + f64(prior)[:1]

@@ -1,0 +1,278 @@
+from contextlib import ExitStack
+
+import concourse.mybir as mybir
+from concourse.masks import make_identity
+
+K, T, S, H, D, V, W, U = 1024, 1024, 512, 512, 8, 128, 2048, 1024
+FLOPS = 2 * K * H * S + 2 * H * S * U
+
+F32 = mybir.dt.float32
+BF16 = mybir.dt.bfloat16
+I32 = mybir.dt.int32
+U32 = mybir.dt.uint32
+U16 = mybir.dt.uint16
+U8 = mybir.dt.uint8
+FP8X4 = mybir.dt.float8_e4m3fn_x4
+ACT = mybir.ActivationFunctionType
+ALU = mybir.AluOpType
+AX = mybir.AxisListType
+
+P = 128
+PACK = 4
+PASSES = K // (P * PACK)
+HALF = 256
+NQ = 4
+QN = U // NQ
+WCH = 2
+WC = H // WCH
+
+
+def tile_picked_yparz_log_p_kernel(
+    tc, x_words, x_scales, w1, e_words, e_scales, half, prior, offs, pro, out
+):
+    nc = tc.nc
+    with ExitStack() as ctx:
+        lists = ctx.enter_context(tc.tile_pool(name="lists", bufs=1))
+        keep = ctx.enter_context(tc.tile_pool(name="keep", bufs=1))
+        ring = ctx.enter_context(tc.tile_pool(name="ring", bufs=4))
+        psum = ctx.enter_context(tc.psum_pool(name="psum", bufs=1))
+
+        offs_sb = lists.tile([P, S // 16], U16, name="offs_sb")
+        pro_sb = lists.tile([P, U // 16], U16, name="pro_sb")
+
+        xs_tab = keep.tile([P, T], U8, name="xs_tab", align_bytes=64)
+        es_tab = keep.tile([P, W], U8, name="es_tab", align_bytes=64)
+        half_tab = keep.tile([P, W], F32, name="half_tab", align_bytes=64)
+        xw_tab = [keep.tile([P, T], U32, name=f"xw_tab{o}", tag=f"xw_tab{o}", align_bytes=64) for o in range(PASSES)]
+        ew_tab = keep.tile([P, W], U32, name="ew_tab", align_bytes=64)
+        prior_sb = keep.tile([P, V], F32, name="prior_sb")
+        ident = keep.tile([P, P], F32, name="ident")
+        w_raw = [[keep.tile([P, PACK, WC], F32, name=f"w_raw{o}_{c}", tag=f"w_raw{o}_{c}") for c in range(WCH)] for o in range(PASSES)]
+
+        nc.gpsimd.memset(xs_tab[:].bitcast(I32), 0)
+        nc.gpsimd.memset(half_tab[:, W // 2 :], 0.0)
+        nc.vector.memset(half_tab[:, : W // 2], 0.0)
+        nc.vector.memset(es_tab[:].bitcast(I32), 0)
+        make_identity(nc, ident[:])
+
+        def load_w(o, c):
+            rows = w1[o * 512 : (o + 1) * 512, c * WC : (c + 1) * WC]
+            nc.sync.dma_start(out=w_raw[o][c][:], in_=rows.rearrange("(p j) c -> p j c", j=PACK))
+
+        def load_x(o):
+            nc.sync.dma_start(
+                out=xw_tab[o][:].bitcast(I32), in_=x_words[o].rearrange("p n r -> p (n r)").bitcast(I32)
+            )
+
+        nc.sync.dma_start(offs_sb[:], offs)
+        nc.sync.dma_start(pro_sb[:], pro)
+        nc.sync.dma_start(out=prior_sb[:], in_=prior)
+        for q in range(4):
+            nc.sync.dma_start(
+                out=xs_tab[32 * q : 32 * q + 8, :].bitcast(I32), in_=x_scales[:, 4 * q : 4 * q + 4, :].bitcast(I32)
+            )
+        load_w(0, 0)
+        nc.sync.dma_start(out=half_tab[0:1, :], in_=half[0:1, :])
+        load_w(0, 1)
+        load_x(0)
+        for q in range(4):
+            nc.sync.dma_start(
+                out=es_tab[32 * q : 32 * q + 4, :].bitcast(I32), in_=e_scales[0, 4 * q : 4 * q + 4, :].bitcast(I32)
+            )
+        load_w(1, 0)
+        load_w(1, 1)
+        load_x(1)
+        nc.sync.dma_start(out=ew_tab[:].bitcast(I32), in_=e_words[0].rearrange("p n r -> p (n r)").bitcast(I32))
+
+        w_codes, w_scales = [], []
+        w_grouped = [keep.tile([P, PACK * H], BF16, name=f"w_grouped{o}", tag=f"w_grouped{o}", align_bytes=64) for o in range(PASSES)]
+
+        def group_w(o, c):
+            ms = slice(c * WC // PACK, (c + 1) * WC // PACK)
+            dst = w_grouped[o][:].rearrange("p (t m j) -> p m j t", t=PACK, j=PACK)
+            nc.scalar.copy(out=dst[:, ms, :, :], in_=w_raw[o][c][:].rearrange("p j (m t) -> p m j t", t=PACK))
+
+        def quant_w(o):
+            codes = keep.tile([P, H], U32, name=f"w_codes{o}", align_bytes=64)
+            scales = keep.tile([P, H], U8, name=f"w_scales{o}", align_bytes=64)
+            nc.vector.quantize_mx(out=codes[:].bitcast(FP8X4), scales=scales[:], in_=w_grouped[o][:])
+            w_codes.append(codes)
+            w_scales.append(scales)
+
+        xs_g = keep.tile([P, S], U8, name="xs_g", align_bytes=64)
+        xw_g = {}
+
+        def gather_xs():
+            nc.vector.tensor_copy(xs_g[:], xs_tab[:].indirect(offs_sb[:]))
+
+        def gather_xw(o, t0, t1, tag):
+            g = keep.tile([P, t1 - t0], U32, name=f"xw_g{o}_{t0}", tag=tag, align_bytes=64)
+            nc.vector.tensor_copy(g[:], xw_tab[o][:].indirect(offs_sb[:, t0 // 16 : t1 // 16]))
+            for b in range(t0 // P, t1 // P):
+                xw_g[o, b] = g[:, b * P - t0 : (b + 1) * P - t0]
+
+        es_p = {}
+        ew_g = {}
+        nbias = {}
+
+        def gather_es(b, tag):
+            g = keep.tile([P, 2 * QN], U8, name=f"es_g{b}", tag=tag, align_bytes=64)
+            nc.vector.tensor_copy(g[:], es_tab[:].indirect(pro_sb[:, b * 32 : (b + 1) * 32]))
+            pm = keep.tile([P, 2 * QN], U8, name=f"es_p{b}", align_bytes=64)
+            nc.vector.tensor_copy(
+                out=pm[:].bitcast(I32).rearrange("p (u h v) -> p u h v", u=2, h=2),
+                in_=g[:].bitcast(I32).rearrange("p (u v h) -> p u h v", u=2, h=2),
+            )
+            for i in range(2):
+                es_p[2 * b + i] = pm[:, i * QN : (i + 1) * QN]
+
+        def gather_ew(u0, n, tag):
+            g = keep.tile([P, n * QN], U32, name=f"ew_g{u0}", tag=tag, align_bytes=64)
+            for i in range(n):
+                ew_g[u0 + i] = g[:, i * QN : (i + 1) * QN]
+                nc.vector.tensor_copy(
+                    ew_g[u0 + i].rearrange("p (h v d) -> p v h d", h=2, d=4),
+                    ew_tab[:].indirect(pro_sb[:, (u0 + i) * 16 : (u0 + i + 1) * 16]),
+                )
+
+        half_g = keep.tile([P, U], F32, name="half_g")
+
+        def gather_half():
+            nc.vector.tensor_copy(half_g[:], half_tab[:].indirect(pro_sb[:]))
+
+        def turn_half():
+            pm = keep.tile([P, U], F32, name="half_p", tag="w_raw1_1")
+            for b in range(2):
+                cols = slice(b * 2 * QN, (b + 1) * 2 * QN)
+                nc.scalar.copy(
+                    out=pm[:, cols].rearrange("p (u h v d) -> p u h v d", u=2, h=2, d=4),
+                    in_=half_g[:, cols].rearrange("p (u v h d) -> p u h v d", u=2, h=2, d=4),
+                )
+            for b in range(2):
+                bank = psum.tile([P, 4, P], F32, name="turn", tag="acc", bufs=2)
+                for i in range(4):
+                    c0 = (4 * b + i) * P
+                    nc.tensor.transpose(bank[:, i, :], pm[:, c0 : c0 + P], ident[:])
+                nb = keep.tile([P, 4], F32, name=f"nbias{b}")
+                nc.scalar.activation(out=nb[:], in_=bank[:, :, 0], func=ACT.Copy, scale=-1.0)
+                for i in range(2):
+                    nbias[2 * b + i] = nb[:, 2 * i : 2 * i + 2]
+
+        pieces = [(0, 256), (256, 512)]
+        h_bf = [
+            keep.tile([P, t1 - t0, PACK], BF16, name=f"h_bf{i}", tag=f"h_bf{i}", align_bytes=64)
+            for i, (t0, t1) in enumerate(pieces)
+        ]
+        h_codes = keep.tile([P, S], U32, name="h_codes", align_bytes=64)
+        h_scales = keep.tile([P, S], U8, name="h_scales", align_bytes=64)
+
+        def first_product(g):
+            bank = psum.tile([P, PACK, P], F32, name="h_bank", tag="prod", bufs=6)
+            cols = slice(g * P, (g + 1) * P)
+            for t in range(PACK):
+                for o in range(PASSES):
+                    nc.tensor.matmul_mx(
+                        out=bank[:, t, :],
+                        lhsT=w_codes[o][:, t * P : (t + 1) * P].bitcast(FP8X4),
+                        lhsT_scale=w_scales[o][:, t * P : (t + 1) * P],
+                        rhs=xw_g[o, g].bitcast(FP8X4),
+                        rhs_scale=xs_g[4 * o : P, cols],
+                        start=(o == 0),
+                        stop=(o == PASSES - 1),
+                    )
+            i = g // 2
+            c0 = g * P - pieces[i][0]
+            nc.scalar.copy(out=h_bf[i][:, c0 : c0 + P, :], in_=bank[:].rearrange("p t n -> p n t"))
+
+        def quant_h(i):
+            t0, t1 = pieces[i]
+            nc.vector.quantize_mx(
+                out=h_codes[:, t0:t1].bitcast(FP8X4),
+                scales=h_scales[:, t0:t1],
+                in_=h_bf[i][:].rearrange("p n t -> p (n t)"),
+            )
+
+        sums = keep.tile([P, 4, V], F32, name="sums")
+        ee = {}
+
+        def second_product(u, t0, t1):
+            n = t1 - t0
+            if n <= HALF:
+                bank = psum.tile([P, 2, n], F32, name="y_bank", tag="prod", bufs=6)
+                y = [bank[:, h, :] for h in range(2)]
+            else:
+                y = [psum.tile([P, n], F32, name="y_bank", tag="prod", bufs=6)[:] for h in range(2)]
+            runs = [(t0, t1)]
+            for h in range(2):
+                for r0, r1 in runs:
+                    nc.tensor.matmul_mx(
+                        out=y[h][:, r0 - t0 : r1 - t0],
+                        lhsT=ew_g[u][:, h * P : (h + 1) * P].bitcast(FP8X4),
+                        lhsT_scale=es_p[u][:, h * P : (h + 1) * P],
+                        rhs=h_codes[:, r0:r1].bitcast(FP8X4),
+                        rhs_scale=h_scales[:, r0:r1],
+                        start=True,
+                        stop=True,
+                    )
+            e = ring.tile([P, 2, n], F32, name="ee", tag="ee", bufs=7)
+            for h in range(2):
+                nc.scalar.activation(out=e[:, h, :], in_=y[h], func=ACT.Exp, bias=nbias[u][:, h : h + 1])
+            ee[u, t0] = e
+
+        def sum_up(u, t0, t1):
+            nb = (t1 - t0) // P
+            bank = psum.tile([P, nb, P], F32, name="acc", tag="acc", bufs=2)
+            for g in range(nb):
+                for h in range(2):
+                    nc.tensor.matmul(
+                        out=bank[:, g, :],
+                        lhsT=ee[u, t0][:, h, g * P : (g + 1) * P],
+                        rhs=ident[:],
+                        start=(h == 0),
+                        stop=(h == 1),
+                        is_transpose=True,
+                    )
+            nc.vector.tensor_reduce(
+                out=sums[:, t0 // P : t1 // P, 32 * u : 32 * (u + 1)],
+                in_=bank[:].rearrange("p g (v d) -> p g v d", d=4),
+                axis=AX.X,
+                op=ALU.add,
+            )
+
+        gather_xs()
+        group_w(0, 0)
+        gather_half()
+        group_w(0, 1)
+        gather_xw(0, 0, S, "xw_g0")
+        quant_w(0)
+        group_w(1, 0)
+        group_w(1, 1)
+        turn_half()
+        gather_xw(1, 0, P, "xw_g1")
+        quant_w(1)
+        gather_xw(1, P, S, "w_grouped1")
+        for g in range(4):
+            first_product(g)
+        gather_es(0, "xw_tab1")
+        gather_ew(0, 1, "ew_g0")
+        quant_h(0)
+        gather_ew(1, 1, "h_bf0")
+        quant_h(1)
+        gather_es(1, "h_bf1")
+        gather_ew(2, 2, "h_bf1")
+        steps = [(0, 0, 256), (1, 0, 256), (0, 256, 512), (1, 256, 512), (2, 0, 512), (3, 0, 256), (3, 256, 512)]
+        for i in range(len(steps) + 2):
+            if i < len(steps):
+                second_product(*steps[i])
+            if i >= 2:
+                sum_up(*steps[i - 2])
+
+        out_v = out.rearrange("(a g p) v -> g p a v", a=2, g=2)
+        for g in range(2):
+            logs = ring.tile([P, 2, V], F32, name="logs")
+            nc.scalar.activation(out=logs[:], in_=sums[:, g::2, :], func=ACT.Ln)
+            res = ring.tile([P, 2, V], F32, name="res")
+            nc.vector.tensor_tensor(
+                out=res[:], in0=logs[:], in1=prior_sb[:].unsqueeze(1).broadcast_to([P, 2, V]), op=ALU.add
+            )
+            nc.sync.dma_start(out=out_v[g], in_=res[:])

@@ -66,14 +66,13 @@ def tile_picked_yparz_log_p_kernel(
 
         nc.sync.dma_start(offs_sb[:], offs)
         nc.sync.dma_start(pro_sb[:], pro)
-        nc.sync.dma_start(out=prior_sb[:], in_=prior)
+        load_w(0, 0)
         for q in range(4):
             nc.sync.dma_start(
                 out=xs_tab[32 * q : 32 * q + 8, :].bitcast(I32), in_=x_scales[:, 4 * q : 4 * q + 4, :].bitcast(I32)
             )
-        load_w(0, 0)
-        nc.sync.dma_start(out=half_tab[0:1, :], in_=half[0:1, :])
         load_w(0, 1)
+        nc.sync.dma_start(out=half_tab[0:1, :], in_=half[0:1, :])
         load_x(0)
         for q in range(4):
             nc.sync.dma_start(
@@ -83,6 +82,7 @@ def tile_picked_yparz_log_p_kernel(
         load_w(1, 1)
         load_x(1)
         nc.sync.dma_start(out=ew_tab[:].bitcast(I32), in_=e_words[0].rearrange("p n r -> p (n r)").bitcast(I32))
+        nc.sync.dma_start(out=prior_sb[:], in_=prior)
 
         w_codes, w_scales = [], []
         w_grouped = [keep.tile([P, PACK * H], BF16, name=f"w_grouped{o}", tag=f"w_grouped{o}", align_bytes=64) for o in range(PASSES)]
@@ -93,7 +93,7 @@ def tile_picked_yparz_log_p_kernel(
             nc.scalar.copy(out=dst[:, ms, :, :], in_=w_raw[o][c][:].rearrange("p j (m t) -> p m j t", t=PACK))
 
         def quant_w(o):
-            codes = keep.tile([P, H], U32, name=f"w_codes{o}", align_bytes=64)
+            codes = keep.tile([P, H], U32, name=f"w_codes{o}", tag="xw_tab0" if o == 0 else "w_codes1", align_bytes=64)
             scales = keep.tile([P, H], U8, name=f"w_scales{o}", align_bytes=64)
             nc.vector.quantize_mx(out=codes[:].bitcast(FP8X4), scales=scales[:], in_=w_grouped[o][:])
             w_codes.append(codes)
@@ -108,6 +108,7 @@ def tile_picked_yparz_log_p_kernel(
         def gather_xw(o, t0, t1, tag):
             g = keep.tile([P, t1 - t0], U32, name=f"xw_g{o}_{t0}", tag=tag, align_bytes=64)
             nc.vector.tensor_copy(g[:], xw_tab[o][:].indirect(offs_sb[:, t0 // 16 : t1 // 16]))
+            xw_g[o, t0, t1] = g
             for b in range(t0 // P, t1 // P):
                 xw_g[o, b] = g[:, b * P - t0 : (b + 1) * P - t0]
 
@@ -140,6 +141,8 @@ def tile_picked_yparz_log_p_kernel(
         def gather_half():
             nc.vector.tensor_copy(half_g[:], half_tab[:].indirect(pro_sb[:]))
 
+        half_p = []
+
         def turn_half():
             pm = keep.tile([P, U], F32, name="half_p", tag="w_raw1_1")
             for b in range(2):
@@ -148,8 +151,12 @@ def tile_picked_yparz_log_p_kernel(
                     out=pm[:, cols].rearrange("p (u h v d) -> p u h v d", u=2, h=2, d=4),
                     in_=half_g[:, cols].rearrange("p (u v h d) -> p u h v d", u=2, h=2, d=4),
                 )
+            half_p.append(pm)
+
+        def turn_half2():
+            pm = half_p[0]
             for b in range(2):
-                bank = psum.tile([P, 4, P], F32, name="turn", tag="acc", bufs=2)
+                bank = psum.tile([P, 4, P], F32, name="turn", tag="prod", bufs=4)
                 for i in range(4):
                     c0 = (4 * b + i) * P
                     nc.tensor.transpose(bank[:, i, :], pm[:, c0 : c0 + P], ident[:])
@@ -167,7 +174,7 @@ def tile_picked_yparz_log_p_kernel(
         h_scales = keep.tile([P, S], U8, name="h_scales", align_bytes=64)
 
         def first_product(g):
-            bank = psum.tile([P, PACK, P], F32, name="h_bank", tag="prod", bufs=6)
+            bank = psum.tile([P, PACK, P], F32, name="h_bank", tag="prod", bufs=4)
             cols = slice(g * P, (g + 1) * P)
             for t in range(PACK):
                 for o in range(PASSES):
@@ -198,10 +205,10 @@ def tile_picked_yparz_log_p_kernel(
         def second_product(u, t0, t1):
             n = t1 - t0
             if n <= HALF:
-                bank = psum.tile([P, 2, n], F32, name="y_bank", tag="prod", bufs=6)
+                bank = psum.tile([P, 2, n], F32, name="y_bank", tag="prod", bufs=4)
                 y = [bank[:, h, :] for h in range(2)]
             else:
-                y = [psum.tile([P, n], F32, name="y_bank", tag="prod", bufs=6)[:] for h in range(2)]
+                y = [psum.tile([P, n], F32, name="y_bank", tag="prod", bufs=4)[:] for h in range(2)]
             runs = [(t0, t1)]
             for h in range(2):
                 for r0, r1 in runs:
@@ -221,7 +228,7 @@ def tile_picked_yparz_log_p_kernel(
 
         def sum_up(u, t0, t1):
             nb = (t1 - t0) // P
-            bank = psum.tile([P, nb, P], F32, name="acc", tag="acc", bufs=2)
+            bank = psum.tile([P, nb, P], F32, name="acc", tag="acc", bufs=4)
             for g in range(nb):
                 for h in range(2):
                     nc.tensor.matmul(
@@ -244,6 +251,17 @@ def tile_picked_yparz_log_p_kernel(
         gather_half()
         group_w(0, 1)
         gather_xw(0, 0, S, "xw_g0")
+        for i in range(3):
+            warm = psum.tile([P, S], F32, name="warm", tag="acc", bufs=4)
+            nc.tensor.matmul_mx(
+                out=warm[:],
+                lhsT=xw_g[0, 0].bitcast(FP8X4),
+                lhsT_scale=xs_g[:, 0:P],
+                rhs=xw_g[0, 0, S][:].bitcast(FP8X4),
+                rhs_scale=xs_g[:],
+                start=True,
+                stop=True,
+            )
         quant_w(0)
         group_w(1, 0)
         group_w(1, 1)
@@ -253,6 +271,7 @@ def tile_picked_yparz_log_p_kernel(
         gather_xw(1, P, S, "w_grouped1")
         for g in range(4):
             first_product(g)
+        turn_half2()
         gather_es(0, "xw_tab1")
         gather_ew(0, 1, "ew_g0")
         quant_h(0)

@@ -23,7 +23,7 @@ PASSES = K // (P * PACK)
 HALF = 256
 NQ = 4
 QN = U // NQ
-WCH = 2
+WCH = 1
 WC = H // WCH
 
 
@@ -49,10 +49,10 @@ def tile_picked_yparz_log_p_kernel(
         ident = keep.tile([P, P], F32, name="ident")
         w_raw = [[keep.tile([P, PACK, WC], F32, name=f"w_raw{o}_{c}", tag=f"w_raw{o}_{c}") for c in range(WCH)] for o in range(PASSES)]
 
-        nc.gpsimd.memset(xs_tab[:].bitcast(I32), 0)
-        nc.gpsimd.memset(half_tab[:, W // 2 :], 0.0)
-        nc.vector.memset(half_tab[:, : W // 2], 0.0)
-        nc.vector.memset(es_tab[:].bitcast(I32), 0)
+        nc.vector.memset(xs_tab[:].bitcast(I32), 0)
+        nc.vector.memset(half_tab[32:64, :], 0.0)
+        nc.gpsimd.memset(half_tab[64:128, :], 0.0)
+        nc.gpsimd.memset(es_tab[:].bitcast(I32), 0)
         make_identity(nc, ident[:])
 
         def load_w(o, c):
@@ -66,20 +66,18 @@ def tile_picked_yparz_log_p_kernel(
 
         nc.sync.dma_start(offs_sb[:], offs)
         nc.sync.dma_start(pro_sb[:], pro)
-        load_w(0, 0)
+        nc.sync.dma_start(out=half_tab[0:32, :], in_=half[0:32, :])
         for q in range(4):
             nc.sync.dma_start(
                 out=xs_tab[32 * q : 32 * q + 8, :].bitcast(I32), in_=x_scales[:, 4 * q : 4 * q + 4, :].bitcast(I32)
             )
-        load_w(0, 1)
-        nc.sync.dma_start(out=half_tab[0:1, :], in_=half[0:1, :])
-        load_x(0)
+        load_w(0, 0)
         for q in range(4):
             nc.sync.dma_start(
                 out=es_tab[32 * q : 32 * q + 4, :].bitcast(I32), in_=e_scales[0, 4 * q : 4 * q + 4, :].bitcast(I32)
             )
         load_w(1, 0)
-        load_w(1, 1)
+        load_x(0)
         load_x(1)
         nc.sync.dma_start(out=ew_tab[:].bitcast(I32), in_=e_words[0].rearrange("p n r -> p (n r)").bitcast(I32))
         nc.sync.dma_start(out=prior_sb[:], in_=prior)
@@ -93,7 +91,7 @@ def tile_picked_yparz_log_p_kernel(
             nc.scalar.copy(out=dst[:, ms, :, :], in_=w_raw[o][c][:].rearrange("p j (m t) -> p m j t", t=PACK))
 
         def quant_w(o):
-            codes = keep.tile([P, H], U32, name=f"w_codes{o}", tag="xw_tab0" if o == 0 else "w_codes1", align_bytes=64)
+            codes = keep.tile([P, H], U32, name=f"w_codes{o}", tag="es_g0" if o == 0 else "w_codes1", align_bytes=64)
             scales = keep.tile([P, H], U8, name=f"w_scales{o}", align_bytes=64)
             nc.vector.quantize_mx(out=codes[:].bitcast(FP8X4), scales=scales[:], in_=w_grouped[o][:])
             w_codes.append(codes)
@@ -113,13 +111,18 @@ def tile_picked_yparz_log_p_kernel(
                 xw_g[o, b] = g[:, b * P - t0 : (b + 1) * P - t0]
 
         es_p = {}
+        es_g = {}
         ew_g = {}
         nbias = {}
 
         def gather_es(b, tag):
             g = keep.tile([P, 2 * QN], U8, name=f"es_g{b}", tag=tag, align_bytes=64)
             nc.vector.tensor_copy(g[:], es_tab[:].indirect(pro_sb[:, b * 32 : (b + 1) * 32]))
-            pm = keep.tile([P, 2 * QN], U8, name=f"es_p{b}", align_bytes=64)
+            es_g[b] = g
+
+        def regroup_es(b, tag):
+            g = es_g[b]
+            pm = keep.tile([P, 2 * QN], U8, name=f"es_p{b}", tag=tag, align_bytes=64)
             nc.vector.tensor_copy(
                 out=pm[:].bitcast(I32).rearrange("p (u h v) -> p u h v", u=2, h=2),
                 in_=g[:].bitcast(I32).rearrange("p (u v h) -> p u h v", u=2, h=2),
@@ -144,7 +147,7 @@ def tile_picked_yparz_log_p_kernel(
         half_p = []
 
         def turn_half():
-            pm = keep.tile([P, U], F32, name="half_p", tag="w_raw1_1")
+            pm = keep.tile([P, U], F32, name="half_p", tag="w_raw1_0")
             for b in range(2):
                 cols = slice(b * 2 * QN, (b + 1) * 2 * QN)
                 nc.scalar.copy(
@@ -246,39 +249,38 @@ def tile_picked_yparz_log_p_kernel(
                 op=ALU.add,
             )
 
-        gather_xs()
-        group_w(0, 0)
         gather_half()
-        group_w(0, 1)
-        gather_xw(0, 0, S, "xw_g0")
+        gather_xs()
+        gather_es(0, "es_g0")
+        regroup_es(0, "es_p0")
+        group_w(0, 0)
+        quant_w(0)
         for i in range(3):
-            warm = psum.tile([P, S], F32, name="warm", tag="acc", bufs=4)
+            warm = psum.tile([P, H], F32, name="warm", tag="acc", bufs=4)
             nc.tensor.matmul_mx(
                 out=warm[:],
-                lhsT=xw_g[0, 0].bitcast(FP8X4),
-                lhsT_scale=xs_g[:, 0:P],
-                rhs=xw_g[0, 0, S][:].bitcast(FP8X4),
-                rhs_scale=xs_g[:],
+                lhsT=w_codes[0][:, 0:P].bitcast(FP8X4),
+                lhsT_scale=w_scales[0][:, 0:P],
+                rhs=w_codes[0][:].bitcast(FP8X4),
+                rhs_scale=w_scales[0][:],
                 start=True,
                 stop=True,
             )
-        quant_w(0)
         group_w(1, 0)
-        group_w(1, 1)
         turn_half()
-        gather_xw(1, 0, P, "xw_g1")
+        gather_xw(0, 0, S, "xw_g0")
         quant_w(1)
-        gather_xw(1, P, S, "w_grouped1")
+        gather_xw(1, 0, P, "xw_g1")
+        gather_xw(1, P, S, "xw_g1_rest")
         for g in range(4):
             first_product(g)
         turn_half2()
-        gather_es(0, "xw_tab1")
-        gather_ew(0, 1, "ew_g0")
+        gather_ew(0, 2, "ew_g0")
         quant_h(0)
-        gather_ew(1, 1, "h_bf0")
+        gather_es(1, "h_bf0")
         quant_h(1)
-        gather_es(1, "h_bf1")
-        gather_ew(2, 2, "h_bf1")
+        regroup_es(1, "h_bf1")
+        gather_ew(2, 2, "h_bf0")
         steps = [(0, 0, 256), (1, 0, 256), (0, 256, 512), (1, 256, 512), (2, 0, 512), (3, 0, 256), (3, 256, 512)]
         for i in range(len(steps) + 2):
             if i < len(steps):

@@ -50,9 +50,9 @@ def tile_picked_yparz_log_p_kernel(
         w_raw = [[keep.tile([P, PACK, WC], F32, name=f"w_raw{o}_{c}", tag=f"w_raw{o}_{c}") for c in range(WCH)] for o in range(PASSES)]
 
         nc.vector.memset(xs_tab[:].bitcast(I32), 0)
-        nc.vector.memset(half_tab[32:64, :], 0.0)
-        nc.gpsimd.memset(half_tab[64:128, :], 0.0)
-        nc.gpsimd.memset(es_tab[:].bitcast(I32), 0)
+        nc.vector.memset(es_tab[:].bitcast(I32), 0)
+        nc.vector.memset(half_tab[32:64, :].bitcast(I32), 0)
+        nc.vector.memset(half_tab[64:128, :].bitcast(I32), 0)
         make_identity(nc, ident[:])
 
         def load_w(o, c):
@@ -159,7 +159,7 @@ def tile_picked_yparz_log_p_kernel(
         def turn_half2():
             pm = half_p[0]
             for b in range(2):
-                bank = psum.tile([P, 4, P], F32, name="turn", tag="prod", bufs=4)
+                bank = psum.tile([P, 4, P], F32, name="turn", tag=f"bank{b}")
                 for i in range(4):
                     c0 = (4 * b + i) * P
                     nc.tensor.transpose(bank[:, i, :], pm[:, c0 : c0 + P], ident[:])
@@ -177,7 +177,7 @@ def tile_picked_yparz_log_p_kernel(
         h_scales = keep.tile([P, S], U8, name="h_scales", align_bytes=64)
 
         def first_product(g):
-            bank = psum.tile([P, PACK, P], F32, name="h_bank", tag="prod", bufs=4)
+            bank = psum.tile([P, PACK, P], F32, name="h_bank", tag=f"bank{g}")
             cols = slice(g * P, (g + 1) * P)
             for t in range(PACK):
                 for o in range(PASSES):
@@ -205,13 +205,13 @@ def tile_picked_yparz_log_p_kernel(
         sums = keep.tile([P, 4, V], F32, name="sums")
         ee = {}
 
-        def second_product(u, t0, t1):
+        def second_product(u, t0, t1, slot):
             n = t1 - t0
             if n <= HALF:
-                bank = psum.tile([P, 2, n], F32, name="y_bank", tag="prod", bufs=4)
+                bank = psum.tile([P, 2, n], F32, name="y_bank", tag=f"bank{slot}")
                 y = [bank[:, h, :] for h in range(2)]
             else:
-                y = [psum.tile([P, n], F32, name="y_bank", tag="prod", bufs=4)[:] for h in range(2)]
+                y = [psum.tile([P, n], F32, name="y_bank", tag=f"bank{slot + h}")[:] for h in range(2)]
             runs = [(t0, t1)]
             for h in range(2):
                 for r0, r1 in runs:
@@ -224,14 +224,14 @@ def tile_picked_yparz_log_p_kernel(
                         start=True,
                         stop=True,
                     )
-            e = ring.tile([P, 2, n], F32, name="ee", tag="ee", bufs=7)
+            e = ring.tile([P, 2, n], F32, name="ee", tag="ee", bufs=8)
             for h in range(2):
                 nc.scalar.activation(out=e[:, h, :], in_=y[h], func=ACT.Exp, bias=nbias[u][:, h : h + 1])
             ee[u, t0] = e
 
-        def sum_up(u, t0, t1):
+        def sum_up(u, t0, t1, slot):
             nb = (t1 - t0) // P
-            bank = psum.tile([P, nb, P], F32, name="acc", tag="acc", bufs=4)
+            bank = psum.tile([P, nb, P], F32, name="acc", tag=f"bank{slot}")
             for g in range(nb):
                 for h in range(2):
                     nc.tensor.matmul(
@@ -256,7 +256,7 @@ def tile_picked_yparz_log_p_kernel(
         group_w(0, 0)
         quant_w(0)
         for i in range(3):
-            warm = psum.tile([P, H], F32, name="warm", tag="acc", bufs=4)
+            warm = psum.tile([P, H], F32, name="warm", tag="bank7")
             nc.tensor.matmul_mx(
                 out=warm[:],
                 lhsT=w_codes[0][:, 0:P].bitcast(FP8X4),
@@ -281,12 +281,20 @@ def tile_picked_yparz_log_p_kernel(
         quant_h(1)
         regroup_es(1, "h_bf1")
         gather_ew(2, 2, "h_bf0")
-        steps = [(0, 0, 256), (1, 0, 256), (0, 256, 512), (1, 256, 512), (2, 0, 512), (3, 0, 256), (3, 256, 512)]
-        for i in range(len(steps) + 2):
-            if i < len(steps):
-                second_product(*steps[i])
-            if i >= 2:
-                sum_up(*steps[i - 2])
+        steps = [(2 * b + i, a * HALF, (a + 1) * HALF) for b, i, a in
+                 [(0, 0, 0), (0, 1, 0), (0, 0, 1), (0, 1, 1), (1, 0, 0), (1, 0, 1), (1, 1, 0), (1, 1, 1)]]
+        y_slot = [4, 5, 6, 7, 5, 6, 7, 5]
+        acc_slot = [0, 1, 2, 3, 4, 0, 1, 2]
+        for i in range(4):
+            second_product(*steps[i], y_slot[i])
+        sum_up(*steps[0], acc_slot[0])
+        sum_up(*steps[1], acc_slot[1])
+        second_product(*steps[4], y_slot[4])
+        for i in range(5, 8):
+            second_product(*steps[i], y_slot[i])
+            sum_up(*steps[i - 3], acc_slot[i - 3])
+        for i in range(5, 8):
+            sum_up(*steps[i], acc_slot[i])
 
         out_v = out.rearrange("(a g p) v -> g p a v", a=2, g=2)
         for g in range(2):

@@ -23,8 +23,7 @@ PASSES = K // (P * PACK)
 HALF = 256
 NQ = 4
 QN = U // NQ
-WCH = 1
-WC = H // WCH
+WARM_UPS = 4
 
 
 def tile_picked_yparz_log_p_kernel(
@@ -34,7 +33,7 @@ def tile_picked_yparz_log_p_kernel(
     with ExitStack() as ctx:
         lists = ctx.enter_context(tc.tile_pool(name="lists", bufs=1))
         keep = ctx.enter_context(tc.tile_pool(name="keep", bufs=1))
-        ring = ctx.enter_context(tc.tile_pool(name="ring", bufs=4))
+        ring = ctx.enter_context(tc.tile_pool(name="ring", bufs=2))
         psum = ctx.enter_context(tc.psum_pool(name="psum", bufs=1))
 
         offs_sb = lists.tile([P, S // 16], U16, name="offs_sb")
@@ -47,36 +46,35 @@ def tile_picked_yparz_log_p_kernel(
         ew_tab = keep.tile([P, W], U32, name="ew_tab", align_bytes=64)
         prior_sb = keep.tile([P, V], F32, name="prior_sb")
         ident = keep.tile([P, P], F32, name="ident")
-        w_raw = [[keep.tile([P, PACK, WC], F32, name=f"w_raw{o}_{c}", tag=f"w_raw{o}_{c}") for c in range(WCH)] for o in range(PASSES)]
+        w_raw = [keep.tile([P, PACK, H], F32, name=f"w_raw{o}", tag=f"w_raw{o}") for o in range(PASSES)]
 
-        nc.vector.memset(xs_tab[:].bitcast(I32), 0)
         nc.vector.memset(es_tab[:].bitcast(I32), 0)
-        nc.vector.memset(half_tab[32:64, :].bitcast(I32), 0)
-        nc.vector.memset(half_tab[64:128, :].bitcast(I32), 0)
+        nc.vector.memset(half_tab[:].bitcast(I32), 0)
+        nc.vector.memset(xs_tab[:].bitcast(I32), 0)
         make_identity(nc, ident[:])
 
-        def load_w(o, c):
-            rows = w1[o * 512 : (o + 1) * 512, c * WC : (c + 1) * WC]
-            nc.sync.dma_start(out=w_raw[o][c][:], in_=rows.rearrange("(p j) c -> p j c", j=PACK))
+        def load_w(o):
+            rows = w1[o * 512 : (o + 1) * 512, :]
+            nc.sync.dma_start(out=w_raw[o][:], in_=rows.rearrange("(p j) c -> p j c", j=PACK))
 
         def load_x(o):
             nc.sync.dma_start(
                 out=xw_tab[o][:].bitcast(I32), in_=x_words[o].rearrange("p n r -> p (n r)").bitcast(I32)
             )
 
-        nc.sync.dma_start(offs_sb[:], offs)
         nc.sync.dma_start(pro_sb[:], pro)
-        nc.sync.dma_start(out=half_tab[0:32, :], in_=half[0:32, :])
-        for q in range(4):
-            nc.sync.dma_start(
-                out=xs_tab[32 * q : 32 * q + 8, :].bitcast(I32), in_=x_scales[:, 4 * q : 4 * q + 4, :].bitcast(I32)
-            )
-        load_w(0, 0)
+        nc.sync.dma_start(offs_sb[:], offs)
         for q in range(4):
             nc.sync.dma_start(
                 out=es_tab[32 * q : 32 * q + 4, :].bitcast(I32), in_=e_scales[0, 4 * q : 4 * q + 4, :].bitcast(I32)
             )
-        load_w(1, 0)
+        load_w(0)
+        nc.sync.dma_start(out=half_tab[0:1, :], in_=half[0:1, :])
+        for q in range(4):
+            nc.sync.dma_start(
+                out=xs_tab[32 * q : 32 * q + 8, :].bitcast(I32), in_=x_scales[:, 4 * q : 4 * q + 4, :].bitcast(I32)
+            )
+        load_w(1)
         load_x(0)
         load_x(1)
         nc.sync.dma_start(out=ew_tab[:].bitcast(I32), in_=e_words[0].rearrange("p n r -> p (n r)").bitcast(I32))
@@ -85,14 +83,13 @@ def tile_picked_yparz_log_p_kernel(
         w_codes, w_scales = [], []
         w_grouped = [keep.tile([P, PACK * H], BF16, name=f"w_grouped{o}", tag=f"w_grouped{o}", align_bytes=64) for o in range(PASSES)]
 
-        def group_w(o, c):
-            ms = slice(c * WC // PACK, (c + 1) * WC // PACK)
+        def group_w(o):
             dst = w_grouped[o][:].rearrange("p (t m j) -> p m j t", t=PACK, j=PACK)
-            nc.scalar.copy(out=dst[:, ms, :, :], in_=w_raw[o][c][:].rearrange("p j (m t) -> p m j t", t=PACK))
+            nc.scalar.copy(out=dst, in_=w_raw[o][:].rearrange("p j (m t) -> p m j t", t=PACK))
 
         def quant_w(o):
-            codes = keep.tile([P, H], U32, name=f"w_codes{o}", tag="es_g0" if o == 0 else "w_codes1", align_bytes=64)
-            scales = keep.tile([P, H], U8, name=f"w_scales{o}", align_bytes=64)
+            codes = keep.tile([P, H], U32, name=f"w_codes{o}", tag=("half_tab", "w_codes1")[o], align_bytes=64)
+            scales = keep.tile([P, H], U8, name=f"w_scales{o}", tag=("xs_tab", "w_scales1")[o], align_bytes=64)
             nc.vector.quantize_mx(out=codes[:].bitcast(FP8X4), scales=scales[:], in_=w_grouped[o][:])
             w_codes.append(codes)
             w_scales.append(scales)
@@ -100,35 +97,19 @@ def tile_picked_yparz_log_p_kernel(
         xs_g = keep.tile([P, S], U8, name="xs_g", align_bytes=64)
         xw_g = {}
 
-        def gather_xs():
-            nc.vector.tensor_copy(xs_g[:], xs_tab[:].indirect(offs_sb[:]))
-
-        def gather_xw(o, t0, t1, tag):
-            g = keep.tile([P, t1 - t0], U32, name=f"xw_g{o}_{t0}", tag=tag, align_bytes=64)
+        def gather_xw(o, t0, t1):
+            g = keep.tile([P, t1 - t0], U32, name=f"xw_g{o}_{t0}", tag=f"xw_g{o}_{t0}", align_bytes=64)
             nc.vector.tensor_copy(g[:], xw_tab[o][:].indirect(offs_sb[:, t0 // 16 : t1 // 16]))
-            xw_g[o, t0, t1] = g
             for b in range(t0 // P, t1 // P):
                 xw_g[o, b] = g[:, b * P - t0 : (b + 1) * P - t0]
 
-        es_p = {}
-        es_g = {}
+        es_g = keep.tile([P, U], U8, name="es_g", align_bytes=64)
+        es_p = keep.tile([P, U], U8, name="es_p", align_bytes=64)
+        half_g = keep.tile([P, U], F32, name="half_g", align_bytes=64)
         ew_g = {}
-        nbias = {}
 
-        def gather_es(b, tag):
-            g = keep.tile([P, 2 * QN], U8, name=f"es_g{b}", tag=tag, align_bytes=64)
-            nc.vector.tensor_copy(g[:], es_tab[:].indirect(pro_sb[:, b * 32 : (b + 1) * 32]))
-            es_g[b] = g
-
-        def regroup_es(b, tag):
-            g = es_g[b]
-            pm = keep.tile([P, 2 * QN], U8, name=f"es_p{b}", tag=tag, align_bytes=64)
-            nc.vector.tensor_copy(
-                out=pm[:].bitcast(I32).rearrange("p (u h v) -> p u h v", u=2, h=2),
-                in_=g[:].bitcast(I32).rearrange("p (u v h) -> p u h v", u=2, h=2),
-            )
-            for i in range(2):
-                es_p[2 * b + i] = pm[:, i * QN : (i + 1) * QN]
+        def dealt_cols(u, h):
+            return slice(h * U // 2 + u * P, h * U // 2 + (u + 1) * P)
 
         def gather_ew(u0, n, tag):
             g = keep.tile([P, n * QN], U32, name=f"ew_g{u0}", tag=tag, align_bytes=64)
@@ -139,40 +120,22 @@ def tile_picked_yparz_log_p_kernel(
                     ew_tab[:].indirect(pro_sb[:, (u0 + i) * 16 : (u0 + i + 1) * 16]),
                 )
 
-        half_g = keep.tile([P, U], F32, name="half_g")
-
-        def gather_half():
-            nc.vector.tensor_copy(half_g[:], half_tab[:].indirect(pro_sb[:]))
-
-        half_p = []
+        def negate_half(banks):
+            nb = keep.tile([P, 2, NQ], F32, name="nbias", tag="w_raw1")
+            for h in range(2):
+                nc.scalar.activation(out=nb[:, h, :], in_=banks[h][:, :, 0], func=ACT.Copy, scale=-1.0)
+            return nb
 
         def turn_half():
-            pm = keep.tile([P, U], F32, name="half_p", tag="w_raw1_0")
-            for b in range(2):
-                cols = slice(b * 2 * QN, (b + 1) * 2 * QN)
-                nc.scalar.copy(
-                    out=pm[:, cols].rearrange("p (u h v d) -> p u h v d", u=2, h=2, d=4),
-                    in_=half_g[:, cols].rearrange("p (u v h d) -> p u h v d", u=2, h=2, d=4),
-                )
-            half_p.append(pm)
+            banks = []
+            for h in range(2):
+                bank = psum.tile([P, NQ, P], F32, name="turn", tag=f"bank{4 + h}")
+                for u in range(NQ):
+                    nc.tensor.transpose(bank[:, u, :], half_g[:, dealt_cols(u, h)], ident[:])
+                banks.append(bank)
+            return banks
 
-        def turn_half2():
-            pm = half_p[0]
-            for b in range(2):
-                bank = psum.tile([P, 4, P], F32, name="turn", tag=f"bank{b}")
-                for i in range(4):
-                    c0 = (4 * b + i) * P
-                    nc.tensor.transpose(bank[:, i, :], pm[:, c0 : c0 + P], ident[:])
-                nb = keep.tile([P, 4], F32, name=f"nbias{b}")
-                nc.scalar.activation(out=nb[:], in_=bank[:, :, 0], func=ACT.Copy, scale=-1.0)
-                for i in range(2):
-                    nbias[2 * b + i] = nb[:, 2 * i : 2 * i + 2]
-
-        pieces = [(0, 256), (256, 512)]
-        h_bf = [
-            keep.tile([P, t1 - t0, PACK], BF16, name=f"h_bf{i}", tag=f"h_bf{i}", align_bytes=64)
-            for i, (t0, t1) in enumerate(pieces)
-        ]
+        h_bf = [keep.tile([P, HALF, PACK], BF16, name=f"h_bf{i}", tag=f"h_bf{i}", align_bytes=64) for i in range(2)]
         h_codes = keep.tile([P, S], U32, name="h_codes", align_bytes=64)
         h_scales = keep.tile([P, S], U8, name="h_scales", align_bytes=64)
 
@@ -190,20 +153,20 @@ def tile_picked_yparz_log_p_kernel(
                         start=(o == 0),
                         stop=(o == PASSES - 1),
                     )
-            i = g // 2
-            c0 = g * P - pieces[i][0]
-            nc.scalar.copy(out=h_bf[i][:, c0 : c0 + P, :], in_=bank[:].rearrange("p t n -> p n t"))
+            c0 = (g % 2) * P
+            copy = nc.vector.tensor_copy if g == 3 else nc.scalar.copy
+            copy(out=h_bf[g // 2][:, c0 : c0 + P, :], in_=bank[:].rearrange("p t n -> p n t"))
 
         def quant_h(i):
-            t0, t1 = pieces[i]
+            cols = slice(i * HALF, (i + 1) * HALF)
             nc.vector.quantize_mx(
-                out=h_codes[:, t0:t1].bitcast(FP8X4),
-                scales=h_scales[:, t0:t1],
+                out=h_codes[:, cols].bitcast(FP8X4),
+                scales=h_scales[:, cols],
                 in_=h_bf[i][:].rearrange("p n t -> p (n t)"),
             )
 
         sums = keep.tile([P, 4, V], F32, name="sums")
-        ee = {}
+        ee = [keep.tile([P, 2, S], F32, name=f"ee{u}", tag=f"ee{u}") for u in range(NQ)]
 
         def second_product(u, t0, t1, slot):
             n = t1 - t0
@@ -212,22 +175,18 @@ def tile_picked_yparz_log_p_kernel(
                 y = [bank[:, h, :] for h in range(2)]
             else:
                 y = [psum.tile([P, n], F32, name="y_bank", tag=f"bank{slot + h}")[:] for h in range(2)]
-            runs = [(t0, t1)]
             for h in range(2):
-                for r0, r1 in runs:
-                    nc.tensor.matmul_mx(
-                        out=y[h][:, r0 - t0 : r1 - t0],
-                        lhsT=ew_g[u][:, h * P : (h + 1) * P].bitcast(FP8X4),
-                        lhsT_scale=es_p[u][:, h * P : (h + 1) * P],
-                        rhs=h_codes[:, r0:r1].bitcast(FP8X4),
-                        rhs_scale=h_scales[:, r0:r1],
-                        start=True,
-                        stop=True,
-                    )
-            e = ring.tile([P, 2, n], F32, name="ee", tag="ee", bufs=8)
+                nc.tensor.matmul_mx(
+                    out=y[h],
+                    lhsT=ew_g[u][:, h * P : (h + 1) * P].bitcast(FP8X4),
+                    lhsT_scale=es_p[:, dealt_cols(u, h)],
+                    rhs=h_codes[:, t0:t1].bitcast(FP8X4),
+                    rhs_scale=h_scales[:, t0:t1],
+                    start=True,
+                    stop=True,
+                )
             for h in range(2):
-                nc.scalar.activation(out=e[:, h, :], in_=y[h], func=ACT.Exp, bias=nbias[u][:, h : h + 1])
-            ee[u, t0] = e
+                nc.scalar.activation(out=ee[u][:, h, t0:t1], in_=y[h], func=ACT.Exp, bias=nbias[:, h, u : u + 1])
 
         def sum_up(u, t0, t1, slot):
             nb = (t1 - t0) // P
@@ -236,7 +195,7 @@ def tile_picked_yparz_log_p_kernel(
                 for h in range(2):
                     nc.tensor.matmul(
                         out=bank[:, g, :],
-                        lhsT=ee[u, t0][:, h, g * P : (g + 1) * P],
+                        lhsT=ee[u][:, h, t0 + g * P : t0 + (g + 1) * P],
                         rhs=ident[:],
                         start=(h == 0),
                         stop=(h == 1),
@@ -249,14 +208,22 @@ def tile_picked_yparz_log_p_kernel(
                 op=ALU.add,
             )
 
-        gather_half()
-        gather_xs()
-        gather_es(0, "es_g0")
-        regroup_es(0, "es_p0")
-        group_w(0, 0)
+        nc.vector.tensor_copy(es_g[:], es_tab[:].indirect(pro_sb[:]))
+        nc.vector.tensor_copy(
+            half_g[:].bitcast(U32).rearrange("p (h v d) -> p v h d", h=2, d=4),
+            half_tab[:].bitcast(U32).indirect(pro_sb[:]),
+        )
+        nc.vector.tensor_copy(
+            out=es_p[:].bitcast(I32).rearrange("p (h v) -> p h v", h=2),
+            in_=es_g[:].bitcast(I32).rearrange("p (v h) -> p h v", h=2),
+        )
+        nc.vector.tensor_copy(xs_g[:], xs_tab[:].indirect(offs_sb[:]))
+        group_w(0)
         quant_w(0)
-        for i in range(3):
-            warm = psum.tile([P, H], F32, name="warm", tag="bank7")
+        group_w(1)
+        turned = turn_half()
+        warm = psum.tile([P, H], F32, name="warm", tag="bank7")
+        for i in range(WARM_UPS):
             nc.tensor.matmul_mx(
                 out=warm[:],
                 lhsT=w_codes[0][:, 0:P].bitcast(FP8X4),
@@ -266,42 +233,38 @@ def tile_picked_yparz_log_p_kernel(
                 start=True,
                 stop=True,
             )
-        group_w(1, 0)
-        turn_half()
-        gather_xw(0, 0, S, "xw_g0")
+        gather_xw(0, 0, S)
         quant_w(1)
-        gather_xw(1, 0, P, "xw_g1")
-        gather_xw(1, P, S, "xw_g1_rest")
-        for g in range(4):
-            first_product(g)
-        turn_half2()
+        gather_xw(1, 0, P)
+        gather_xw(1, P, S)
+        nbias = negate_half(turned)
+        first_product(0)
+        first_product(1)
+        first_product(2)
+        first_product(3)
         gather_ew(0, 2, "ew_g0")
         quant_h(0)
-        gather_es(1, "h_bf0")
         quant_h(1)
-        regroup_es(1, "h_bf1")
-        gather_ew(2, 2, "h_bf0")
-        steps = [(2 * b + i, a * HALF, (a + 1) * HALF) for b, i, a in
-                 [(0, 0, 0), (0, 1, 0), (0, 0, 1), (0, 1, 1), (1, 0, 0), (1, 0, 1), (1, 1, 0), (1, 1, 1)]]
-        y_slot = [4, 5, 6, 7, 5, 6, 7, 5]
-        acc_slot = [0, 1, 2, 3, 4, 0, 1, 2]
-        for i in range(4):
-            second_product(*steps[i], y_slot[i])
-        sum_up(*steps[0], acc_slot[0])
-        sum_up(*steps[1], acc_slot[1])
-        second_product(*steps[4], y_slot[4])
-        for i in range(5, 8):
-            second_product(*steps[i], y_slot[i])
-            sum_up(*steps[i - 3], acc_slot[i - 3])
-        for i in range(5, 8):
-            sum_up(*steps[i], acc_slot[i])
+        gather_ew(2, 2, "h_bf1")
+        second_product(0, 0, HALF, 4)
+        second_product(1, 0, HALF, 5)
+        second_product(0, HALF, S, 6)
+        second_product(1, HALF, S, 7)
+        second_product(2, 0, S, 0)
+        second_product(3, 0, HALF, 2)
+        second_product(3, HALF, S, 3)
+        sum_up(0, 0, S, 4)
+        sum_up(1, 0, S, 5)
+        sum_up(2, 0, S, 6)
+        sum_up(3, 0, HALF, 7)
+        sum_up(3, HALF, S, 0)
 
-        out_v = out.rearrange("(a g p) v -> g p a v", a=2, g=2)
-        for g in range(2):
+        out_v = out.rearrange("(a g p) v -> a p g v", a=2, g=2)
+        for a in range(2):
             logs = ring.tile([P, 2, V], F32, name="logs")
-            nc.scalar.activation(out=logs[:], in_=sums[:, g::2, :], func=ACT.Ln)
+            nc.scalar.activation(out=logs[:], in_=sums[:, 2 * a : 2 * a + 2, :], func=ACT.Ln)
             res = ring.tile([P, 2, V], F32, name="res")
             nc.vector.tensor_tensor(
                 out=res[:], in0=logs[:], in1=prior_sb[:].unsqueeze(1).broadcast_to([P, 2, V]), op=ALU.add
             )
-            nc.sync.dma_start(out=out_v[g], in_=res[:])
+            nc.sync.dma_start(out=out_v[a], in_=res[:])

@@ -51,7 +51,8 @@ def tile_picked_yparz_log_p_kernel(
         nc.vector.memset(es_tab[:].bitcast(I32), 0)
         nc.vector.memset(half_tab[:].bitcast(I32), 0)
         nc.vector.memset(xs_tab[:].bitcast(I32), 0)
-        make_identity(nc, ident[:])
+        nc.vector.memset(ident[:], 0.0)
+        make_identity(nc, ident[:], nomemset=True)
 
         def load_w(o):
             rows = w1[o * 512 : (o + 1) * 512, :]
@@ -236,7 +237,8 @@ def tile_picked_yparz_log_p_kernel(
         gather_xw(0, 0, S)
         quant_w(1)
         gather_xw(1, 0, P)
-        gather_xw(1, P, S)
+        gather_xw(1, P, HALF)
+        gather_xw(1, HALF, S)
         nbias = negate_half(turned)
         first_product(0)
         first_product(1)

@@ -24,6 +24,7 @@ HALF = 256
 NQ = 4
 QN = U // NQ
 WARM_UPS = 4
+HALF_ROW = 16
 
 
 def tile_picked_yparz_log_p_kernel(
@@ -33,7 +34,7 @@ def tile_picked_yparz_log_p_kernel(
     with ExitStack() as ctx:
         lists = ctx.enter_context(tc.tile_pool(name="lists", bufs=1))
         keep = ctx.enter_context(tc.tile_pool(name="keep", bufs=1))
-        ring = ctx.enter_context(tc.tile_pool(name="ring", bufs=2))
+        ring = ctx.enter_context(tc.tile_pool(name="ring", bufs=4))
         psum = ctx.enter_context(tc.psum_pool(name="psum", bufs=1))
 
         offs_sb = lists.tile([P, S // 16], U16, name="offs_sb")
@@ -70,7 +71,7 @@ def tile_picked_yparz_log_p_kernel(
                 out=es_tab[32 * q : 32 * q + 4, :].bitcast(I32), in_=e_scales[0, 4 * q : 4 * q + 4, :].bitcast(I32)
             )
         load_w(0)
-        nc.sync.dma_start(out=half_tab[0:1, :], in_=half[0:1, :])
+        nc.sync.dma_start(out=half_tab[HALF_ROW : HALF_ROW + 1, :], in_=half[0:1, :])
         for q in range(4):
             nc.sync.dma_start(
                 out=xs_tab[32 * q : 32 * q + 8, :].bitcast(I32), in_=x_scales[:, 4 * q : 4 * q + 4, :].bitcast(I32)
@@ -124,7 +125,7 @@ def tile_picked_yparz_log_p_kernel(
         def negate_half(banks):
             nb = keep.tile([P, 2, NQ], F32, name="nbias", tag="w_raw1")
             for h in range(2):
-                nc.scalar.activation(out=nb[:, h, :], in_=banks[h][:, :, 0], func=ACT.Copy, scale=-1.0)
+                nc.scalar.activation(out=nb[:, h, :], in_=banks[h][:, :, HALF_ROW], func=ACT.Copy, scale=-1.0)
             return nb
 
         def turn_half():
@@ -155,7 +156,7 @@ def tile_picked_yparz_log_p_kernel(
                         stop=(o == PASSES - 1),
                     )
             c0 = (g % 2) * P
-            copy = nc.vector.tensor_copy if g == 3 else nc.scalar.copy
+            copy = nc.scalar.copy
             copy(out=h_bf[g // 2][:, c0 : c0 + P, :], in_=bank[:].rearrange("p t n -> p n t"))
 
         def quant_h(i):
@@ -261,12 +262,9 @@ def tile_picked_yparz_log_p_kernel(
         sum_up(3, 0, HALF, 7)
         sum_up(3, HALF, S, 0)
 
-        out_v = out.rearrange("(a g p) v -> a p g v", a=2, g=2)
-        for a in range(2):
-            logs = ring.tile([P, 2, V], F32, name="logs")
-            nc.scalar.activation(out=logs[:], in_=sums[:, 2 * a : 2 * a + 2, :], func=ACT.Ln)
-            res = ring.tile([P, 2, V], F32, name="res")
-            nc.vector.tensor_tensor(
-                out=res[:], in0=logs[:], in1=prior_sb[:].unsqueeze(1).broadcast_to([P, 2, V]), op=ALU.add
-            )
-            nc.sync.dma_start(out=out_v[a], in_=res[:])
+        for g in range(4):
+            logs = ring.tile([P, V], F32, name="logs")
+            nc.scalar.activation(out=logs[:], in_=sums[:, g, :], func=ACT.Ln)
+            res = ring.tile([P, V], F32, name="res")
+            nc.vector.tensor_tensor(out=res[:], in0=logs[:], in1=prior_sb[:], op=ALU.add)
+            nc.sync.dma_start(out=out[g * P : (g + 1) * P, :], in_=res[:])

@@ -91,7 +91,7 @@ def tile_picked_yparz_log_p_kernel(
 
         def quant_w(o):
             codes = keep.tile([P, H], U32, name=f"w_codes{o}", tag=("half_tab", "w_codes1")[o], align_bytes=64)
-            scales = keep.tile([P, H], U8, name=f"w_scales{o}", tag=("xs_tab", "w_scales1")[o], align_bytes=64)
+            scales = keep.tile([P, H], U8, name=f"w_scales{o}", tag=f"w_scales{o}", align_bytes=64)
             nc.vector.quantize_mx(out=codes[:].bitcast(FP8X4), scales=scales[:], in_=w_grouped[o][:])
             w_codes.append(codes)
             w_scales.append(scales)
@@ -106,7 +106,6 @@ def tile_picked_yparz_log_p_kernel(
                 xw_g[o, b] = g[:, b * P - t0 : (b + 1) * P - t0]
 
         es_g = keep.tile([P, U], U8, name="es_g", align_bytes=64)
-        es_p = keep.tile([P, U], U8, name="es_p", align_bytes=64)
         half_g = keep.tile([P, U], F32, name="half_g", align_bytes=64)
         ew_g = {}
 
@@ -215,13 +214,9 @@ def tile_picked_yparz_log_p_kernel(
             half_g[:].bitcast(U32).rearrange("p (h v d) -> p v h d", h=2, d=4),
             half_tab[:].bitcast(U32).indirect(pro_sb[:]),
         )
-        nc.vector.tensor_copy(
-            out=es_p[:].bitcast(I32).rearrange("p (h v) -> p h v", h=2),
-            in_=es_g[:].bitcast(I32).rearrange("p (v h) -> p h v", h=2),
-        )
-        nc.vector.tensor_copy(xs_g[:], xs_tab[:].indirect(offs_sb[:]))
         group_w(0)
         quant_w(0)
+        nc.vector.tensor_copy(xs_g[:], xs_tab[:].indirect(offs_sb[:]))
         group_w(1)
         turned = turn_half()
         warm = psum.tile([P, H], F32, name="warm", tag="bank7")
@@ -231,7 +226,7 @@ def tile_picked_yparz_log_p_kernel(
                 lhsT=w_codes[0][:, 0:P].bitcast(FP8X4),
                 lhsT_scale=w_scales[0][:, 0:P],
                 rhs=w_codes[0][:].bitcast(FP8X4),
-                rhs_scale=w_scales[0][:],
+                rhs_scale=(w_scales[0] if i < WARM_UPS // 2 else xs_g)[:],
                 start=True,
                 stop=True,
             )
@@ -240,6 +235,11 @@ def tile_picked_yparz_log_p_kernel(
         gather_xw(1, 0, P)
         gather_xw(1, P, HALF)
         gather_xw(1, HALF, S)
+        es_p = keep.tile([P, U], U8, name="es_p", tag="w_grouped1", align_bytes=64)
+        nc.vector.tensor_copy(
+            out=es_p[:].bitcast(I32).rearrange("p (h v) -> p h v", h=2),
+            in_=es_g[:].bitcast(I32).rearrange("p (v h) -> p h v", h=2),
+        )
         nbias = negate_half(turned)
         first_product(0)
         first_product(1)

@@ -82,28 +82,36 @@ def tile_picked_yparz_log_p_kernel(
         nc.sync.dma_start(out=ew_tab[:].bitcast(I32), in_=e_words[0].rearrange("p n r -> p (n r)").bitcast(I32))
         nc.sync.dma_start(out=prior_sb[:], in_=prior)
 
-        w_codes, w_scales = [], []
-        w_grouped = [keep.tile([P, PACK * H], BF16, name=f"w_grouped{o}", tag=f"w_grouped{o}", align_bytes=64) for o in range(PASSES)]
+        w_codes, w_scales, w_grouped = {}, {}, {}
 
-        def group_w(o):
-            dst = w_grouped[o][:].rearrange("p (t m j) -> p m j t", t=PACK, j=PACK)
-            nc.scalar.copy(out=dst, in_=w_raw[o][:].rearrange("p j (m t) -> p m j t", t=PACK))
+        def group_w(o, t0, t1):
+            n = t1 - t0
+            g = keep.tile([P, n * H], BF16, name=f"w_grouped{o}_{t0}", tag=f"w_grouped{o}_{t0}", align_bytes=64)
+            src = w_raw[o][:].rearrange("p j (m t) -> p m j t", t=PACK)[:, :, :, t0:t1]
+            nc.scalar.copy(out=g[:].rearrange("p (t m j) -> p m j t", t=n, j=PACK), in_=src)
+            w_grouped[o, t0] = g
 
-        def quant_w(o):
-            codes = keep.tile([P, H], U32, name=f"w_codes{o}", tag=("half_tab", "w_codes1")[o], align_bytes=64)
-            scales = keep.tile([P, H], U8, name=f"w_scales{o}", tag=f"w_scales{o}", align_bytes=64)
-            nc.vector.quantize_mx(out=codes[:].bitcast(FP8X4), scales=scales[:], in_=w_grouped[o][:])
-            w_codes.append(codes)
-            w_scales.append(scales)
+        def quant_w(o, t0, t1, codes_tag):
+            n = t1 - t0
+            codes = keep.tile([P, n * P], U32, name=f"w_codes{o}_{t0}", tag=codes_tag, align_bytes=64)
+            scales = keep.tile([P, n * P], U8, name=f"w_scales{o}_{t0}", tag=f"w_scales{o}_{t0}", align_bytes=64)
+            nc.vector.quantize_mx(out=codes[:].bitcast(FP8X4), scales=scales[:], in_=w_grouped[o, t0][:])
+            for t in range(t0, t1):
+                w_codes[o, t] = codes[:, (t - t0) * P : (t - t0 + 1) * P]
+                w_scales[o, t] = scales[:, (t - t0) * P : (t - t0 + 1) * P]
+            return codes, scales
 
         xs_g = keep.tile([P, S], U8, name="xs_g", align_bytes=64)
         xw_g = {}
 
-        def gather_xw(o, t0, t1):
-            g = keep.tile([P, t1 - t0], U32, name=f"xw_g{o}_{t0}", tag=f"xw_g{o}_{t0}", align_bytes=64)
-            nc.vector.tensor_copy(g[:], xw_tab[o][:].indirect(offs_sb[:, t0 // 16 : t1 // 16]))
-            for b in range(t0 // P, t1 // P):
-                xw_g[o, b] = g[:, b * P - t0 : (b + 1) * P - t0]
+        def xw_tile(o, g0, g1, tag):
+            tile = keep.tile([P, (g1 - g0) * P], U32, name=f"xw_g{o}_{g0}", tag=tag, align_bytes=64)
+            for g in range(g0, g1):
+                xw_g[o, g] = tile[:, (g - g0) * P : (g - g0 + 1) * P]
+            return tile
+
+        def gather_xw(o, g0, g1, dst):
+            nc.vector.tensor_copy(dst, xw_tab[o][:].indirect(offs_sb[:, g0 * 8 : g1 * 8]))
 
         es_g = keep.tile([P, U], U8, name="es_g", align_bytes=64)
         half_g = keep.tile([P, U], F32, name="half_g", align_bytes=64)
@@ -140,23 +148,23 @@ def tile_picked_yparz_log_p_kernel(
         h_codes = keep.tile([P, S], U32, name="h_codes", align_bytes=64)
         h_scales = keep.tile([P, S], U8, name="h_scales", align_bytes=64)
 
-        def first_product(g):
-            bank = psum.tile([P, PACK, P], F32, name="h_bank", tag=f"bank{g}")
-            cols = slice(g * P, (g + 1) * P)
+        h_bank = [psum.tile([P, PACK, P], F32, name="h_bank", tag=f"bank{g}") for g in range(4)]
+
+        def first_product(o, g):
             for t in range(PACK):
-                for o in range(PASSES):
-                    nc.tensor.matmul_mx(
-                        out=bank[:, t, :],
-                        lhsT=w_codes[o][:, t * P : (t + 1) * P].bitcast(FP8X4),
-                        lhsT_scale=w_scales[o][:, t * P : (t + 1) * P],
-                        rhs=xw_g[o, g].bitcast(FP8X4),
-                        rhs_scale=xs_g[4 * o : P, cols],
-                        start=(o == 0),
-                        stop=(o == PASSES - 1),
-                    )
+                nc.tensor.matmul_mx(
+                    out=h_bank[g][:, t, :],
+                    lhsT=w_codes[o, t].bitcast(FP8X4),
+                    lhsT_scale=w_scales[o, t],
+                    rhs=xw_g[o, g].bitcast(FP8X4),
+                    rhs_scale=xs_g[4 * o : P, g * P : (g + 1) * P],
+                    start=(o == 0 and t == 0),
+                    stop=(o == PASSES - 1 and t == PACK - 1),
+                )
+
+        def copy_h(g):
             c0 = (g % 2) * P
-            copy = nc.scalar.copy
-            copy(out=h_bf[g // 2][:, c0 : c0 + P, :], in_=bank[:].rearrange("p t n -> p n t"))
+            nc.scalar.copy(out=h_bf[g // 2][:, c0 : c0 + P, :], in_=h_bank[g][:].rearrange("p t n -> p n t"))
 
         def quant_h(i):
             cols = slice(i * HALF, (i + 1) * HALF)
@@ -214,37 +222,44 @@ def tile_picked_yparz_log_p_kernel(
             half_g[:].bitcast(U32).rearrange("p (h v d) -> p v h d", h=2, d=4),
             half_tab[:].bitcast(U32).indirect(pro_sb[:]),
         )
-        group_w(0)
-        quant_w(0)
+        group_w(0, 0, 4)
+        codes0, scales0 = quant_w(0, 0, 4, "half_tab")
         nc.vector.tensor_copy(xs_g[:], xs_tab[:].indirect(offs_sb[:]))
-        group_w(1)
+        group_w(1, 0, 2)
+        group_w(1, 2, 4)
         turned = turn_half()
         warm = psum.tile([P, H], F32, name="warm", tag="bank7")
         for i in range(WARM_UPS):
             nc.tensor.matmul_mx(
                 out=warm[:],
-                lhsT=w_codes[0][:, 0:P].bitcast(FP8X4),
-                lhsT_scale=w_scales[0][:, 0:P],
-                rhs=w_codes[0][:].bitcast(FP8X4),
-                rhs_scale=(w_scales[0] if i < WARM_UPS // 2 else xs_g)[:],
+                lhsT=codes0[:, 0:P].bitcast(FP8X4),
+                lhsT_scale=scales0[:, 0:P],
+                rhs=codes0[:].bitcast(FP8X4),
+                rhs_scale=(scales0 if i < WARM_UPS // 2 else xs_g)[:],
                 start=True,
                 stop=True,
             )
-        gather_xw(0, 0, S)
-        quant_w(1)
-        gather_xw(1, 0, P)
-        gather_xw(1, P, HALF)
-        gather_xw(1, HALF, S)
-        es_p = keep.tile([P, U], U8, name="es_p", tag="w_grouped1", align_bytes=64)
+        quant_w(1, 0, 2, "w_codes1_0")
+        gather_xw(0, 0, 2, xw_tile(0, 0, 2, "xw_g0")[:])
+        quant_w(1, 2, 4, "w_codes1_2")
+        xw_tile(0, 2, 4, "w_grouped1_2")
+        for g in range(4):
+            if g >= 2:
+                gather_xw(0, g, g + 1, xw_g[0, g])
+            gather_xw(1, g, g + 1, xw_tile(1, g, g + 1, f"xw_g1_{g}")[:])
+        es_p = keep.tile([P, U], U8, name="es_p", tag="xw_tab0", align_bytes=64)
         nc.vector.tensor_copy(
             out=es_p[:].bitcast(I32).rearrange("p (h v) -> p h v", h=2),
             in_=es_g[:].bitcast(I32).rearrange("p (v h) -> p h v", h=2),
         )
         nbias = negate_half(turned)
-        first_product(0)
-        first_product(1)
-        first_product(2)
-        first_product(3)
+        first_product(0, 0)
+        first_product(0, 1)
+        for g in range(4):
+            if g >= 2:
+                first_product(0, g)
+            first_product(1, g)
+            copy_h(g)
         gather_ew(0, 2, "ew_g0")
         quant_h(0)
         quant_h(1)

@@ -1,7 +1,6 @@
 from contextlib import ExitStack
 
 import concourse.mybir as mybir
-from concourse.masks import make_identity
 
 K, T, S, H, D, V, W, U = 1024, 1024, 512, 512, 8, 128, 2048, 1024
 FLOPS = 2 * K * H * S + 2 * H * S * U
@@ -23,8 +22,7 @@ PASSES = K // (P * PACK)
 HALF = 256
 NQ = 4
 QN = U // NQ
-WARM_UPS = 4
-HALF_ROW = 16
+HALF_ROW = P - 1
 
 
 def tile_picked_yparz_log_p_kernel(
@@ -49,11 +47,14 @@ def tile_picked_yparz_log_p_kernel(
         ident = keep.tile([P, P], F32, name="ident")
         w_raw = [keep.tile([P, PACK, H], F32, name=f"w_raw{o}", tag=f"w_raw{o}") for o in range(PASSES)]
 
+        diff = keep.tile([P, P], F32, name="diff")
+        dist = keep.tile([P, P], F32, name="dist", align_bytes=64)
+        nc.gpsimd.iota(diff[:], [[-1, P]], base=0, channel_multiplier=1, allow_small_or_imprecise_dtypes=True)
+        nc.scalar.activation(out=dist[:], in_=diff[:], func=ACT.Abs)
+        nc.scalar.activation(out=ident[:], in_=dist[:], func=ACT.Relu, scale=-1.0, bias=1.0)
         nc.vector.memset(es_tab[:].bitcast(I32), 0)
-        nc.vector.memset(half_tab[:].bitcast(I32), 0)
+        nc.vector.memset(half_tab[:HALF_ROW, :].bitcast(I32), 0)
         nc.vector.memset(xs_tab[:].bitcast(I32), 0)
-        nc.vector.memset(ident[:], 0.0)
-        make_identity(nc, ident[:], nomemset=True)
 
         def load_w(o):
             rows = w1[o * 512 : (o + 1) * 512, :]
@@ -64,31 +65,31 @@ def tile_picked_yparz_log_p_kernel(
                 out=xw_tab[o][:].bitcast(I32), in_=x_words[o].rearrange("p n r -> p (n r)").bitcast(I32)
             )
 
-        nc.sync.dma_start(pro_sb[:], pro)
         nc.sync.dma_start(offs_sb[:], offs)
+        load_x(0)
+        nc.sync.dma_start(pro_sb[:], pro)
+        nc.sync.dma_start(out=half_tab[HALF_ROW : HALF_ROW + 1, :], in_=half[0:1, :])
         for q in range(4):
             nc.sync.dma_start(
                 out=es_tab[32 * q : 32 * q + 4, :].bitcast(I32), in_=e_scales[0, 4 * q : 4 * q + 4, :].bitcast(I32)
             )
         load_w(0)
-        nc.sync.dma_start(out=half_tab[HALF_ROW : HALF_ROW + 1, :], in_=half[0:1, :])
         for q in range(4):
             nc.sync.dma_start(
                 out=xs_tab[32 * q : 32 * q + 8, :].bitcast(I32), in_=x_scales[:, 4 * q : 4 * q + 4, :].bitcast(I32)
             )
         load_w(1)
-        load_x(0)
         load_x(1)
         nc.sync.dma_start(out=ew_tab[:].bitcast(I32), in_=e_words[0].rearrange("p n r -> p (n r)").bitcast(I32))
         nc.sync.dma_start(out=prior_sb[:], in_=prior)
 
         w_codes, w_scales, w_grouped = {}, {}, {}
 
-        def group_w(o, t0, t1):
+        def group_w(o, t0, t1, copy):
             n = t1 - t0
             g = keep.tile([P, n * H], BF16, name=f"w_grouped{o}_{t0}", tag=f"w_grouped{o}_{t0}", align_bytes=64)
             src = w_raw[o][:].rearrange("p j (m t) -> p m j t", t=PACK)[:, :, :, t0:t1]
-            nc.scalar.copy(out=g[:].rearrange("p (t m j) -> p m j t", t=n, j=PACK), in_=src)
+            copy(out=g[:].rearrange("p (t m j) -> p m j t", t=n, j=PACK), in_=src)
             w_grouped[o, t0] = g
 
         def quant_w(o, t0, t1, codes_tag):
@@ -113,19 +114,26 @@ def tile_picked_yparz_log_p_kernel(
         def gather_xw(o, g0, g1, dst):
             nc.vector.tensor_copy(dst, xw_tab[o][:].indirect(offs_sb[:, g0 * 8 : g1 * 8]))
 
-        es_g = keep.tile([P, U], U8, name="es_g", align_bytes=64)
-        half_g = keep.tile([P, U], F32, name="half_g", align_bytes=64)
+        es_g = {}
+        half_g = keep.tile([P, U], F32, name="half_g", tag="dist", align_bytes=64)
         ew_g = {}
 
-        def dealt_cols(u, h):
-            return slice(h * U // 2 + u * P, h * U // 2 + (u + 1) * P)
+        def gather_es(i, tag):
+            n = U // 2
+            g = keep.tile([P, n], U8, name=f"es_g{i}", tag=tag, align_bytes=64)
+            nc.vector.tensor_copy(
+                g[:].rearrange("p (h m) -> p m h", h=2), es_tab[:].indirect(pro_sb[:, i * n // 16 : (i + 1) * n // 16])
+            )
+            for u in range(2):
+                for h in range(2):
+                    es_g[2 * i + u, h] = g[:, h * QN + u * P : h * QN + (u + 1) * P]
 
         def gather_ew(u0, n, tag):
             g = keep.tile([P, n * QN], U32, name=f"ew_g{u0}", tag=tag, align_bytes=64)
             for i in range(n):
                 ew_g[u0 + i] = g[:, i * QN : (i + 1) * QN]
                 nc.vector.tensor_copy(
-                    ew_g[u0 + i].rearrange("p (h v d) -> p v h d", h=2, d=4),
+                    ew_g[u0 + i].rearrange("p (h m) -> p m h", h=2),
                     ew_tab[:].indirect(pro_sb[:, (u0 + i) * 16 : (u0 + i + 1) * 16]),
                 )
 
@@ -140,13 +148,12 @@ def tile_picked_yparz_log_p_kernel(
             for h in range(2):
                 bank = psum.tile([P, NQ, P], F32, name="turn", tag=f"bank{4 + h}")
                 for u in range(NQ):
-                    nc.tensor.transpose(bank[:, u, :], half_g[:, dealt_cols(u, h)], ident[:])
+                    nc.tensor.transpose(bank[:, u, :], half_g[:, u * QN + h : (u + 1) * QN : 2], ident[:])
                 banks.append(bank)
             return banks
 
         h_bf = [keep.tile([P, HALF, PACK], BF16, name=f"h_bf{i}", tag=f"h_bf{i}", align_bytes=64) for i in range(2)]
-        h_codes = keep.tile([P, S], U32, name="h_codes", align_bytes=64)
-        h_scales = keep.tile([P, S], U8, name="h_scales", align_bytes=64)
+        h_codes, h_scales = {}, {}
 
         h_bank = [psum.tile([P, PACK, P], F32, name="h_bank", tag=f"bank{g}") for g in range(4)]
 
@@ -166,120 +173,111 @@ def tile_picked_yparz_log_p_kernel(
             c0 = (g % 2) * P
             nc.scalar.copy(out=h_bf[g // 2][:, c0 : c0 + P, :], in_=h_bank[g][:].rearrange("p t n -> p n t"))
 
-        def quant_h(i):
-            cols = slice(i * HALF, (i + 1) * HALF)
+        def quant_h(i, codes_tag):
+            h_codes[i] = keep.tile([P, HALF], U32, name=f"h_codes{i}", tag=codes_tag, align_bytes=64)
+            h_scales[i] = keep.tile([P, HALF], U8, name=f"h_scales{i}", tag=f"h_scales{i}", align_bytes=64)
             nc.vector.quantize_mx(
-                out=h_codes[:, cols].bitcast(FP8X4),
-                scales=h_scales[:, cols],
+                out=h_codes[i][:].bitcast(FP8X4),
+                scales=h_scales[i][:],
                 in_=h_bf[i][:].rearrange("p n t -> p (n t)"),
             )
 
         sums = keep.tile([P, 4, V], F32, name="sums")
         ee = [keep.tile([P, 2, S], F32, name=f"ee{u}", tag=f"ee{u}") for u in range(NQ)]
 
-        def second_product(u, t0, t1, slot):
-            n = t1 - t0
-            if n <= HALF:
-                bank = psum.tile([P, 2, n], F32, name="y_bank", tag=f"bank{slot}")
-                y = [bank[:, h, :] for h in range(2)]
-            else:
-                y = [psum.tile([P, n], F32, name="y_bank", tag=f"bank{slot + h}")[:] for h in range(2)]
+        def second_product(u, i, slot):
+            bank = psum.tile([P, 2, HALF], F32, name="y_bank", tag=f"bank{slot}")
             for h in range(2):
                 nc.tensor.matmul_mx(
-                    out=y[h],
+                    out=bank[:, h, :],
                     lhsT=ew_g[u][:, h * P : (h + 1) * P].bitcast(FP8X4),
-                    lhsT_scale=es_p[:, dealt_cols(u, h)],
-                    rhs=h_codes[:, t0:t1].bitcast(FP8X4),
-                    rhs_scale=h_scales[:, t0:t1],
+                    lhsT_scale=es_g[u, h],
+                    rhs=h_codes[i][:].bitcast(FP8X4),
+                    rhs_scale=h_scales[i][:],
                     start=True,
                     stop=True,
                 )
             for h in range(2):
-                nc.scalar.activation(out=ee[u][:, h, t0:t1], in_=y[h], func=ACT.Exp, bias=nbias[:, h, u : u + 1])
+                nc.scalar.activation(
+                    out=ee[u][:, h, i * HALF : (i + 1) * HALF],
+                    in_=bank[:, h, :],
+                    func=ACT.Exp,
+                    bias=nbias[:, h, u : u + 1],
+                )
 
-        def sum_up(u, t0, t1, slot):
-            nb = (t1 - t0) // P
-            bank = psum.tile([P, nb, P], F32, name="acc", tag=f"bank{slot}")
-            for g in range(nb):
-                for h in range(2):
-                    nc.tensor.matmul(
-                        out=bank[:, g, :],
-                        lhsT=ee[u][:, h, t0 + g * P : t0 + (g + 1) * P],
-                        rhs=ident[:],
-                        start=(h == 0),
-                        stop=(h == 1),
-                        is_transpose=True,
-                    )
+        def sum_up(u0, u1, i, slot):
+            n = u1 - u0
+            bank = psum.tile([P, 2, n, P], F32, name="acc", tag=f"bank{slot}")
+            for u in range(u0, u1):
+                for g in range(2):
+                    t0 = i * HALF + g * P
+                    for h in range(2):
+                        nc.tensor.matmul(
+                            out=bank[:, g, u - u0, :],
+                            lhsT=ee[u][:, h, t0 : t0 + P],
+                            rhs=ident[:],
+                            start=(h == 0),
+                            stop=(h == 1),
+                            is_transpose=True,
+                        )
             nc.vector.tensor_reduce(
-                out=sums[:, t0 // P : t1 // P, 32 * u : 32 * (u + 1)],
-                in_=bank[:].rearrange("p g (v d) -> p g v d", d=4),
+                out=sums[:, 2 * i : 2 * i + 2, 32 * u0 : 32 * u1],
+                in_=bank[:].rearrange("p g u (v d) -> p g (u v) d", d=4),
                 axis=AX.X,
                 op=ALU.add,
             )
 
-        nc.vector.tensor_copy(es_g[:], es_tab[:].indirect(pro_sb[:]))
-        nc.vector.tensor_copy(
-            half_g[:].bitcast(U32).rearrange("p (h v d) -> p v h d", h=2, d=4),
-            half_tab[:].bitcast(U32).indirect(pro_sb[:]),
-        )
-        group_w(0, 0, 4)
-        codes0, scales0 = quant_w(0, 0, 4, "half_tab")
-        nc.vector.tensor_copy(xs_g[:], xs_tab[:].indirect(offs_sb[:]))
-        group_w(1, 0, 2)
-        group_w(1, 2, 4)
-        turned = turn_half()
-        warm = psum.tile([P, H], F32, name="warm", tag="bank7")
-        for i in range(WARM_UPS):
-            nc.tensor.matmul_mx(
-                out=warm[:],
-                lhsT=codes0[:, 0:P].bitcast(FP8X4),
-                lhsT_scale=scales0[:, 0:P],
-                rhs=codes0[:].bitcast(FP8X4),
-                rhs_scale=(scales0 if i < WARM_UPS // 2 else xs_g)[:],
-                start=True,
-                stop=True,
+        def gather_half(i):
+            n = U // 2
+            nc.scalar.activation(
+                out=half_g[:, i * n : (i + 1) * n],
+                in_=half_tab[:].indirect(pro_sb[:, i * n // 16 : (i + 1) * n // 16]),
+                func=ACT.Copy,
             )
-        quant_w(1, 0, 2, "w_codes1_0")
-        gather_xw(0, 0, 2, xw_tile(0, 0, 2, "xw_g0")[:])
+
+        gather_xw(0, 0, 4, xw_tile(0, 0, 4, "xw_g0")[:])
+        gather_es(0, "es_g0")
+        gather_es(1, "es_g1")
+        gather_half(0)
+        gather_half(1)
+        group_w(0, 0, 2, nc.scalar.copy)
+        group_w(0, 2, 4, nc.scalar.copy)
+        nc.vector.tensor_copy(xs_g[:], xs_tab[:].indirect(offs_sb[:]))
+        quant_w(0, 0, 2, "xs_tab")
+        quant_w(0, 2, 4, "w_grouped0_0")
+        group_w(1, 0, 2, nc.scalar.copy)
+        group_w(1, 2, 4, nc.vector.tensor_copy)
         quant_w(1, 2, 4, "w_codes1_2")
-        xw_tile(0, 2, 4, "w_grouped1_2")
+        quant_w(1, 0, 2, "w_codes1_0")
+        turned = turn_half()
+        gather_xw(1, 0, 1, xw_tile(1, 0, 1, "xw_g1_0")[:])
+        xw_tile(1, 1, 4, "w_grouped1_0")
+        for g in range(1, 4):
+            gather_xw(1, g, g + 1, xw_g[1, g])
         for g in range(4):
-            if g >= 2:
-                gather_xw(0, g, g + 1, xw_g[0, g])
-            gather_xw(1, g, g + 1, xw_tile(1, g, g + 1, f"xw_g1_{g}")[:])
-        es_p = keep.tile([P, U], U8, name="es_p", tag="xw_tab0", align_bytes=64)
-        nc.vector.tensor_copy(
-            out=es_p[:].bitcast(I32).rearrange("p (h v) -> p h v", h=2),
-            in_=es_g[:].bitcast(I32).rearrange("p (v h) -> p h v", h=2),
-        )
+            first_product(0, g)
         nbias = negate_half(turned)
-        first_product(0, 0)
-        first_product(0, 1)
         for g in range(4):
-            if g >= 2:
-                first_product(0, g)
             first_product(1, g)
             copy_h(g)
-        gather_ew(0, 2, "ew_g0")
-        quant_h(0)
-        quant_h(1)
-        gather_ew(2, 2, "h_bf1")
-        second_product(0, 0, HALF, 4)
-        second_product(1, 0, HALF, 5)
-        second_product(0, HALF, S, 6)
-        second_product(1, HALF, S, 7)
-        second_product(2, 0, S, 0)
-        second_product(3, 0, HALF, 2)
-        second_product(3, HALF, S, 3)
-        sum_up(0, 0, S, 4)
-        sum_up(1, 0, S, 5)
-        sum_up(2, 0, S, 6)
-        sum_up(3, 0, HALF, 7)
-        sum_up(3, HALF, S, 0)
+        quant_h(0, "h_codes0")
+        for u in range(NQ):
+            gather_ew(u, 1, f"ew_g{u}")
+        quant_h(1, "ew_tab")
+        for i in range(2):
+            for u in range(NQ):
+                second_product(u, i, (4 + 4 * i + u) % 8)
+        sum_up(0, 2, 0, 5)
+        sum_up(2, 4, 0, 7)
+        sum_up(0, 2, 1, 4)
+        sum_up(2, 3, 1, 6)
+        sum_up(3, 4, 1, 0)
 
+        res_first = keep.tile([P, 2, V], F32, name="res_first", tag="ee3")
+        res_second = keep.tile([P, 2, V], F32, name="res_second")
         for g in range(4):
             logs = ring.tile([P, V], F32, name="logs")
             nc.scalar.activation(out=logs[:], in_=sums[:, g, :], func=ACT.Ln)
-            res = ring.tile([P, V], F32, name="res")
-            nc.vector.tensor_tensor(out=res[:], in0=logs[:], in1=prior_sb[:], op=ALU.add)
-            nc.sync.dma_start(out=out[g * P : (g + 1) * P, :], in_=res[:])
+            res = (res_first if g < 2 else res_second)[:, g % 2, :]
+            nc.vector.tensor_tensor(out=res, in0=logs[:], in1=prior_sb[:], op=ALU.add)
+            nc.sync.dma_start(out=out[g * P : (g + 1) * P, :], in_=res)

@@ -33,6 +33,7 @@ def tile_picked_yparz_log_p_kernel(
         lists = ctx.enter_context(tc.tile_pool(name="lists", bufs=1))
         keep = ctx.enter_context(tc.tile_pool(name="keep", bufs=1))
         ring = ctx.enter_context(tc.tile_pool(name="ring", bufs=4))
+        late = ctx.enter_context(tc.tile_pool(name="late", bufs=1))
         psum = ctx.enter_context(tc.psum_pool(name="psum", bufs=1))
 
         offs_sb = lists.tile([P, S // 16], U16, name="offs_sb")
@@ -52,9 +53,9 @@ def tile_picked_yparz_log_p_kernel(
         nc.gpsimd.iota(diff[:], [[-1, P]], base=0, channel_multiplier=1, allow_small_or_imprecise_dtypes=True)
         nc.scalar.activation(out=dist[:], in_=diff[:], func=ACT.Abs)
         nc.scalar.activation(out=ident[:], in_=dist[:], func=ACT.Relu, scale=-1.0, bias=1.0)
-        nc.vector.memset(es_tab[:].bitcast(I32), 0)
-        nc.vector.memset(half_tab[:HALF_ROW, :].bitcast(I32), 0)
         nc.vector.memset(xs_tab[:].bitcast(I32), 0)
+        nc.vector.memset(half_tab[:HALF_ROW, :].bitcast(I32), 0)
+        nc.vector.memset(es_tab[:].bitcast(I32), 0)
 
         def load_w(o):
             rows = w1[o * 512 : (o + 1) * 512, :]
@@ -71,26 +72,30 @@ def tile_picked_yparz_log_p_kernel(
         nc.sync.dma_start(out=half_tab[HALF_ROW : HALF_ROW + 1, :], in_=half[0:1, :])
         for q in range(4):
             nc.sync.dma_start(
-                out=es_tab[32 * q : 32 * q + 4, :].bitcast(I32), in_=e_scales[0, 4 * q : 4 * q + 4, :].bitcast(I32)
+                out=xs_tab[32 * q : 32 * q + 8, :].bitcast(I32), in_=x_scales[:, 4 * q : 4 * q + 4, :].bitcast(I32)
             )
         load_w(0)
         for q in range(4):
             nc.sync.dma_start(
-                out=xs_tab[32 * q : 32 * q + 8, :].bitcast(I32), in_=x_scales[:, 4 * q : 4 * q + 4, :].bitcast(I32)
+                out=es_tab[32 * q : 32 * q + 4, :].bitcast(I32), in_=e_scales[0, 4 * q : 4 * q + 4, :].bitcast(I32)
             )
         load_w(1)
         load_x(1)
         nc.sync.dma_start(out=ew_tab[:].bitcast(I32), in_=e_words[0].rearrange("p n r -> p (n r)").bitcast(I32))
-        nc.sync.dma_start(out=prior_sb[:], in_=prior)
+        prior_in = late.tile([P, 1408], F32, name="prior_in", align_bytes=64, offset=0)
+        nc.sync.dma_start(out=prior_in[:, :V], in_=prior)
+        nc.gpsimd.tensor_copy(prior_sb[:], prior_in[:, :V])
 
         w_codes, w_scales, w_grouped = {}, {}, {}
 
-        def group_w(o, t0, t1, copy):
-            n = t1 - t0
-            g = keep.tile([P, n * H], BF16, name=f"w_grouped{o}_{t0}", tag=f"w_grouped{o}_{t0}", align_bytes=64)
-            src = w_raw[o][:].rearrange("p j (m t) -> p m j t", t=PACK)[:, :, :, t0:t1]
-            copy(out=g[:].rearrange("p (t m j) -> p m j t", t=n, j=PACK), in_=src)
-            w_grouped[o, t0] = g
+        def group_w(o, pair, m0, m1, copy):
+            if (o, pair) not in w_grouped:
+                w_grouped[o, pair] = keep.tile(
+                    [P, 2 * H], BF16, name=f"w_grouped{o}_{pair}", tag=f"w_grouped{o}_{pair}", align_bytes=64
+                )
+            dst = w_grouped[o, pair][:].rearrange("p (t m j) -> p m j t", t=2, j=PACK)[:, m0:m1]
+            src = w_raw[o][:].rearrange("p j (m t) -> p m j t", t=PACK)[:, m0:m1, :, pair : pair + 2]
+            copy(out=dst, in_=src)
 
         def quant_w(o, t0, t1, codes_tag):
             n = t1 - t0
@@ -118,9 +123,8 @@ def tile_picked_yparz_log_p_kernel(
         half_g = keep.tile([P, U], F32, name="half_g", tag="dist", align_bytes=64)
         ew_g = {}
 
-        def gather_es(i, tag):
+        def gather_es(i, g):
             n = U // 2
-            g = keep.tile([P, n], U8, name=f"es_g{i}", tag=tag, align_bytes=64)
             nc.vector.tensor_copy(
                 g[:].rearrange("p (h m) -> p m h", h=2), es_tab[:].indirect(pro_sb[:, i * n // 16 : (i + 1) * n // 16])
             )
@@ -128,14 +132,11 @@ def tile_picked_yparz_log_p_kernel(
                 for h in range(2):
                     es_g[2 * i + u, h] = g[:, h * QN + u * P : h * QN + (u + 1) * P]
 
-        def gather_ew(u0, n, tag):
-            g = keep.tile([P, n * QN], U32, name=f"ew_g{u0}", tag=tag, align_bytes=64)
-            for i in range(n):
-                ew_g[u0 + i] = g[:, i * QN : (i + 1) * QN]
-                nc.vector.tensor_copy(
-                    ew_g[u0 + i].rearrange("p (h m) -> p m h", h=2),
-                    ew_tab[:].indirect(pro_sb[:, (u0 + i) * 16 : (u0 + i + 1) * 16]),
-                )
+        def gather_ew(u, g):
+            ew_g[u] = g[:]
+            nc.vector.tensor_copy(
+                g[:].rearrange("p (h m) -> p m h", h=2), ew_tab[:].indirect(pro_sb[:, u * 16 : (u + 1) * 16])
+            )
 
         def negate_half(banks):
             nb = keep.tile([P, 2, NQ], F32, name="nbias", tag="w_raw1")
@@ -158,23 +159,24 @@ def tile_picked_yparz_log_p_kernel(
         h_bank = [psum.tile([P, PACK, P], F32, name="h_bank", tag=f"bank{g}") for g in range(4)]
 
         def first_product(o, g):
-            for t in range(PACK):
+            order = (2, 3, 0, 1) if o == 0 else (0, 1, 2, 3)
+            for t in order:
                 nc.tensor.matmul_mx(
                     out=h_bank[g][:, t, :],
                     lhsT=w_codes[o, t].bitcast(FP8X4),
                     lhsT_scale=w_scales[o, t],
                     rhs=xw_g[o, g].bitcast(FP8X4),
                     rhs_scale=xs_g[4 * o : P, g * P : (g + 1) * P],
-                    start=(o == 0 and t == 0),
-                    stop=(o == PASSES - 1 and t == PACK - 1),
+                    start=(o == 0 and t == order[0]),
+                    stop=(o == PASSES - 1 and t == order[-1]),
                 )
 
         def copy_h(g):
             c0 = (g % 2) * P
             nc.scalar.copy(out=h_bf[g // 2][:, c0 : c0 + P, :], in_=h_bank[g][:].rearrange("p t n -> p n t"))
 
-        def quant_h(i, codes_tag):
-            h_codes[i] = keep.tile([P, HALF], U32, name=f"h_codes{i}", tag=codes_tag, align_bytes=64)
+        def quant_h(i, codes):
+            h_codes[i] = codes
             h_scales[i] = keep.tile([P, HALF], U8, name=f"h_scales{i}", tag=f"h_scales{i}", align_bytes=64)
             nc.vector.quantize_mx(
                 out=h_codes[i][:].bitcast(FP8X4),
@@ -236,40 +238,41 @@ def tile_picked_yparz_log_p_kernel(
             )
 
         gather_xw(0, 0, 4, xw_tile(0, 0, 4, "xw_g0")[:])
-        gather_es(0, "es_g0")
-        gather_es(1, "es_g1")
+        nc.vector.tensor_copy(xs_g[:], xs_tab[:].indirect(offs_sb[:]))
         gather_half(0)
         gather_half(1)
-        group_w(0, 0, 2, nc.scalar.copy)
-        group_w(0, 2, 4, nc.scalar.copy)
-        nc.vector.tensor_copy(xs_g[:], xs_tab[:].indirect(offs_sb[:]))
-        quant_w(0, 0, 2, "xs_tab")
-        quant_w(0, 2, 4, "w_grouped0_0")
-        group_w(1, 0, 2, nc.scalar.copy)
-        group_w(1, 2, 4, nc.vector.tensor_copy)
-        quant_w(1, 2, 4, "w_codes1_2")
+        group_w(0, 0, 0, P, nc.scalar.copy)
+        group_w(0, 2, 0, P, nc.vector.tensor_copy)
+        quant_w(0, 2, 4, "w_codes0_2")
+        quant_w(0, 0, 2, "w_codes0_0")
+        gather_es(0, keep.tile([P, U // 2], U8, name="es_g0", align_bytes=64))
+        group_w(1, 0, 0, P, nc.scalar.copy)
+        group_w(1, 2, P // 2, P, nc.vector.tensor_copy)
+        group_w(1, 2, 0, P // 2, nc.scalar.copy)
         quant_w(1, 0, 2, "w_codes1_0")
+        gather_xw(1, 0, 2, xw_tile(1, 0, 2, "xw_g1_0")[:])
+        quant_w(1, 2, 4, "w_codes1_2")
         turned = turn_half()
-        gather_xw(1, 0, 1, xw_tile(1, 0, 1, "xw_g1_0")[:])
-        xw_tile(1, 1, 4, "w_grouped1_0")
-        for g in range(1, 4):
-            gather_xw(1, g, g + 1, xw_g[1, g])
+        gather_xw(1, 2, 4, xw_tile(1, 2, 4, "w_grouped1_2")[:])
         for g in range(4):
             first_product(0, g)
         nbias = negate_half(turned)
         for g in range(4):
             first_product(1, g)
             copy_h(g)
-        quant_h(0, "h_codes0")
-        for u in range(NQ):
-            gather_ew(u, 1, f"ew_g{u}")
-        quant_h(1, "ew_tab")
-        for i in range(2):
-            for u in range(NQ):
-                second_product(u, i, (4 + 4 * i + u) % 8)
+        gather_ew(0, keep.tile([P, QN], U32, name="ew_g0", align_bytes=64))
+        quant_h(0, late.tile([P, HALF], U32, name="h_codes0", align_bytes=64, offset=0))
+        gather_ew(1, late.tile([P, QN], U32, name="ew_g1", align_bytes=64, offset=4608))
+        gather_ew(2, late.tile([P, QN], U32, name="ew_g2", align_bytes=64, offset=1024))
+        quant_h(1, late.tile([P, HALF], U32, name="h_codes1", align_bytes=64, offset=2048))
+        gather_es(1, late.tile([P, U // 2], U8, name="es_g1", align_bytes=64, offset=4096))
+        gather_ew(3, late.tile([P, QN], U32, name="ew_g3", align_bytes=64, offset=3072))
+        steps = [(u0 + u, i) for u0 in (0, 2) for i in range(2) for u in range(2)]
+        for n, (u, i) in enumerate(steps):
+            second_product(u, i, (4 + n) % 8)
         sum_up(0, 2, 0, 5)
-        sum_up(2, 4, 0, 7)
-        sum_up(0, 2, 1, 4)
+        sum_up(0, 2, 1, 7)
+        sum_up(2, 4, 0, 4)
         sum_up(2, 3, 1, 6)
         sum_up(3, 4, 1, 0)
 

@@ -22,6 +22,7 @@ PASSES = K // (P * PACK)
 HALF = 256
 NQ = 4
 QN = U // NQ
+ES_ROW = P - 16
 HALF_ROW = P - 1
 
 
@@ -53,9 +54,12 @@ def tile_picked_yparz_log_p_kernel(
         nc.gpsimd.iota(diff[:], [[-1, P]], base=0, channel_multiplier=1, allow_small_or_imprecise_dtypes=True)
         nc.scalar.activation(out=dist[:], in_=diff[:], func=ACT.Abs)
         nc.scalar.activation(out=ident[:], in_=dist[:], func=ACT.Relu, scale=-1.0, bias=1.0)
+        es_g = keep.tile([P, U], U8, name="es_g", align_bytes=64)
+        es_p = keep.tile([P, U], U8, name="es_p", align_bytes=64)
         nc.vector.memset(xs_tab[:].bitcast(I32), 0)
+        nc.vector.memset(es_tab[:ES_ROW, :].bitcast(I32), 0)
         nc.vector.memset(half_tab[:HALF_ROW, :].bitcast(I32), 0)
-        nc.vector.memset(es_tab[:].bitcast(I32), 0)
+        nc.vector.memset(es_p[:].bitcast(I32), 0)
 
         def load_w(o):
             rows = w1[o * 512 : (o + 1) * 512, :]
@@ -66,23 +70,20 @@ def tile_picked_yparz_log_p_kernel(
                 out=xw_tab[o][:].bitcast(I32), in_=x_words[o].rearrange("p n r -> p (n r)").bitcast(I32)
             )
 
-        nc.sync.dma_start(offs_sb[:], offs)
-        load_x(0)
         nc.sync.dma_start(pro_sb[:], pro)
+        nc.sync.dma_start(out=es_tab[ES_ROW:, :].bitcast(I32), in_=e_scales[0].bitcast(I32))
+        nc.sync.dma_start(offs_sb[:], offs)
         nc.sync.dma_start(out=half_tab[HALF_ROW : HALF_ROW + 1, :], in_=half[0:1, :])
+        load_x(0)
         for q in range(4):
             nc.sync.dma_start(
                 out=xs_tab[32 * q : 32 * q + 8, :].bitcast(I32), in_=x_scales[:, 4 * q : 4 * q + 4, :].bitcast(I32)
             )
         load_w(0)
-        for q in range(4):
-            nc.sync.dma_start(
-                out=es_tab[32 * q : 32 * q + 4, :].bitcast(I32), in_=e_scales[0, 4 * q : 4 * q + 4, :].bitcast(I32)
-            )
         load_w(1)
         load_x(1)
         nc.sync.dma_start(out=ew_tab[:].bitcast(I32), in_=e_words[0].rearrange("p n r -> p (n r)").bitcast(I32))
-        prior_in = late.tile([P, 1408], F32, name="prior_in", align_bytes=64, offset=0)
+        prior_in = late.tile([P, 768], F32, name="prior_in", align_bytes=64, offset=0)
         nc.sync.dma_start(out=prior_in[:, :V], in_=prior)
         nc.gpsimd.tensor_copy(prior_sb[:], prior_in[:, :V])
 
@@ -119,23 +120,21 @@ def tile_picked_yparz_log_p_kernel(
         def gather_xw(o, g0, g1, dst):
             nc.vector.tensor_copy(dst, xw_tab[o][:].indirect(offs_sb[:, g0 * 8 : g1 * 8]))
 
-        es_g = {}
         half_g = keep.tile([P, U], F32, name="half_g", tag="dist", align_bytes=64)
         ew_g = {}
 
-        def gather_es(i, g):
-            n = U // 2
-            nc.vector.tensor_copy(
-                g[:].rearrange("p (h m) -> p m h", h=2), es_tab[:].indirect(pro_sb[:, i * n // 16 : (i + 1) * n // 16])
-            )
-            for u in range(2):
-                for h in range(2):
-                    es_g[2 * i + u, h] = g[:, h * QN + u * P : h * QN + (u + 1) * P]
+        def gather_es():
+            nc.vector.tensor_copy(es_g[:].rearrange("p (h m) -> p m h", h=2), es_tab[:].indirect(pro_sb[:]))
+            for q in range(4):
+                nc.sync.dma_start(
+                    out=es_p[32 * q : 32 * q + 4, :].bitcast(I32),
+                    in_=es_g[ES_ROW + 4 * q : ES_ROW + 4 * q + 4, :].bitcast(I32),
+                )
 
         def gather_ew(u, g):
-            ew_g[u] = g[:]
+            ew_g[u] = g
             nc.vector.tensor_copy(
-                g[:].rearrange("p (h m) -> p m h", h=2), ew_tab[:].indirect(pro_sb[:, u * 16 : (u + 1) * 16])
+                g.rearrange("p (h m) -> p m h", h=2), ew_tab[:].indirect(pro_sb[:, u * 16 : (u + 1) * 16])
             )
 
         def negate_half(banks):
@@ -154,12 +153,13 @@ def tile_picked_yparz_log_p_kernel(
             return banks
 
         h_bf = [keep.tile([P, HALF, PACK], BF16, name=f"h_bf{i}", tag=f"h_bf{i}", align_bytes=64) for i in range(2)]
-        h_codes, h_scales = {}, {}
+        h_codes = late.tile([P, S], U32, name="h_codes", align_bytes=64, offset=0)
+        h_scales = keep.tile([P, S], U8, name="h_scales", align_bytes=64)
 
         h_bank = [psum.tile([P, PACK, P], F32, name="h_bank", tag=f"bank{g}") for g in range(4)]
 
         def first_product(o, g):
-            order = (2, 3, 0, 1) if o == 0 else (0, 1, 2, 3)
+            order = (0, 1, 2, 3)
             for t in order:
                 nc.tensor.matmul_mx(
                     out=h_bank[g][:, t, :],
@@ -175,37 +175,36 @@ def tile_picked_yparz_log_p_kernel(
             c0 = (g % 2) * P
             nc.scalar.copy(out=h_bf[g // 2][:, c0 : c0 + P, :], in_=h_bank[g][:].rearrange("p t n -> p n t"))
 
-        def quant_h(i, codes):
-            h_codes[i] = codes
-            h_scales[i] = keep.tile([P, HALF], U8, name=f"h_scales{i}", tag=f"h_scales{i}", align_bytes=64)
+        def quant_h(i):
+            cols = slice(i * HALF, (i + 1) * HALF)
             nc.vector.quantize_mx(
-                out=h_codes[i][:].bitcast(FP8X4),
-                scales=h_scales[i][:],
+                out=h_codes[:, cols].bitcast(FP8X4),
+                scales=h_scales[:, cols],
                 in_=h_bf[i][:].rearrange("p n t -> p (n t)"),
             )
 
         sums = keep.tile([P, 4, V], F32, name="sums")
         ee = [keep.tile([P, 2, S], F32, name=f"ee{u}", tag=f"ee{u}") for u in range(NQ)]
 
-        def second_product(u, i, slot):
-            bank = psum.tile([P, 2, HALF], F32, name="y_bank", tag=f"bank{slot}")
+        def second_product(u, t0, t1, slots):
+            n = t1 - t0
+            if len(slots) == 1:
+                bank = psum.tile([P, 2, n], F32, name="y_bank", tag=f"bank{slots[0]}")
+                y = [bank[:, h, :] for h in range(2)]
+            else:
+                y = [psum.tile([P, n], F32, name="y_bank", tag=f"bank{slots[h]}")[:] for h in range(2)]
             for h in range(2):
                 nc.tensor.matmul_mx(
-                    out=bank[:, h, :],
+                    out=y[h],
                     lhsT=ew_g[u][:, h * P : (h + 1) * P].bitcast(FP8X4),
-                    lhsT_scale=es_g[u, h],
-                    rhs=h_codes[i][:].bitcast(FP8X4),
-                    rhs_scale=h_scales[i][:],
+                    lhsT_scale=es_p[:, h * U // 2 + u * P : h * U // 2 + (u + 1) * P],
+                    rhs=h_codes[:, t0:t1].bitcast(FP8X4),
+                    rhs_scale=h_scales[:, t0:t1],
                     start=True,
                     stop=True,
                 )
             for h in range(2):
-                nc.scalar.activation(
-                    out=ee[u][:, h, i * HALF : (i + 1) * HALF],
-                    in_=bank[:, h, :],
-                    func=ACT.Exp,
-                    bias=nbias[:, h, u : u + 1],
-                )
+                nc.scalar.activation(out=ee[u][:, h, t0:t1], in_=y[h], func=ACT.Exp, bias=nbias[:, h, u : u + 1])
 
         def sum_up(u0, u1, i, slot):
             n = u1 - u0
@@ -237,15 +236,15 @@ def tile_picked_yparz_log_p_kernel(
                 func=ACT.Copy,
             )
 
+        gather_es()
         gather_xw(0, 0, 4, xw_tile(0, 0, 4, "xw_g0")[:])
         nc.vector.tensor_copy(xs_g[:], xs_tab[:].indirect(offs_sb[:]))
         gather_half(0)
         gather_half(1)
         group_w(0, 0, 0, P, nc.scalar.copy)
-        group_w(0, 2, 0, P, nc.vector.tensor_copy)
-        quant_w(0, 2, 4, "w_codes0_2")
+        group_w(0, 2, 0, P, nc.scalar.copy)
         quant_w(0, 0, 2, "w_codes0_0")
-        gather_es(0, keep.tile([P, U // 2], U8, name="es_g0", align_bytes=64))
+        quant_w(0, 2, 4, "w_codes0_2")
         group_w(1, 0, 0, P, nc.scalar.copy)
         group_w(1, 2, P // 2, P, nc.vector.tensor_copy)
         group_w(1, 2, 0, P // 2, nc.scalar.copy)
@@ -260,21 +259,25 @@ def tile_picked_yparz_log_p_kernel(
         for g in range(4):
             first_product(1, g)
             copy_h(g)
-        gather_ew(0, keep.tile([P, QN], U32, name="ew_g0", align_bytes=64))
-        quant_h(0, late.tile([P, HALF], U32, name="h_codes0", align_bytes=64, offset=0))
-        gather_ew(1, late.tile([P, QN], U32, name="ew_g1", align_bytes=64, offset=4608))
-        gather_ew(2, late.tile([P, QN], U32, name="ew_g2", align_bytes=64, offset=1024))
-        quant_h(1, late.tile([P, HALF], U32, name="h_codes1", align_bytes=64, offset=2048))
-        gather_es(1, late.tile([P, U // 2], U8, name="es_g1", align_bytes=64, offset=4096))
-        gather_ew(3, late.tile([P, QN], U32, name="ew_g3", align_bytes=64, offset=3072))
-        steps = [(u0 + u, i) for u0 in (0, 2) for i in range(2) for u in range(2)]
-        for n, (u, i) in enumerate(steps):
-            second_product(u, i, (4 + n) % 8)
-        sum_up(0, 2, 0, 5)
-        sum_up(0, 2, 1, 7)
-        sum_up(2, 4, 0, 4)
-        sum_up(2, 3, 1, 6)
-        sum_up(3, 4, 1, 0)
+        gather_ew(0, keep.tile([P, QN], U32, name="ew_g0", align_bytes=64)[:])
+        quant_h(0)
+        gather_ew(1, late.tile([P, QN], U32, name="ew_g1", align_bytes=64, offset=2048)[:])
+        quant_h(1)
+        ew_last = keep.tile([P, 2 * QN], U32, name="ew_last", tag="h_bf1", align_bytes=64)
+        gather_ew(2, ew_last[:, :QN])
+        gather_ew(3, ew_last[:, QN:])
+        second_product(0, 0, HALF, (4, 5))
+        second_product(1, 0, HALF, (6,))
+        second_product(0, HALF, S, (7, 0))
+        second_product(1, HALF, S, (1,))
+        second_product(2, 0, S, (2, 3))
+        second_product(3, 0, HALF, (4,))
+        second_product(3, HALF, S, (5,))
+        sum_up(0, 2, 0, 6)
+        sum_up(0, 2, 1, 1)
+        sum_up(2, 4, 0, 7)
+        sum_up(2, 3, 1, 0)
+        sum_up(3, 4, 1, 2)
 
         res_first = keep.tile([P, 2, V], F32, name="res_first", tag="ee3")
         res_second = keep.tile([P, 2, V], F32, name="res_second")

@@ -19,11 +19,14 @@ AX = mybir.AxisListType
 P = 128
 PACK = 4
 PASSES = K // (P * PACK)
-HALF = 256
+BLOCKS = S // P
+HALF = S // 2
+SIDES = 2
 NQ = 4
 QN = U // NQ
 ES_ROW = P - 16
 HALF_ROW = P - 1
+TURN_STEP = 16
 
 
 def tile_picked_yparz_log_p_kernel(
@@ -37,253 +40,242 @@ def tile_picked_yparz_log_p_kernel(
         late = ctx.enter_context(tc.tile_pool(name="late", bufs=1))
         psum = ctx.enter_context(tc.psum_pool(name="psum", bufs=1))
 
+        def sb(shape, dtype, name, tag=None):
+            return keep.tile(shape, dtype, name=name, tag=tag or name, align_bytes=64)
+
+        def bank(shape, name, slot):
+            return psum.tile(shape, F32, name=name, tag=f"bank{slot}")
+
         offs_sb = lists.tile([P, S // 16], U16, name="offs_sb")
         pro_sb = lists.tile([P, U // 16], U16, name="pro_sb")
 
-        xs_tab = keep.tile([P, T], U8, name="xs_tab", align_bytes=64)
-        es_tab = keep.tile([P, W], U8, name="es_tab", align_bytes=64)
-        half_tab = keep.tile([P, W], F32, name="half_tab", align_bytes=64)
-        xw_tab = [keep.tile([P, T], U32, name=f"xw_tab{o}", tag=f"xw_tab{o}", align_bytes=64) for o in range(PASSES)]
-        ew_tab = keep.tile([P, W], U32, name="ew_tab", align_bytes=64)
-        prior_sb = keep.tile([P, V], F32, name="prior_sb")
-        ident = keep.tile([P, P], F32, name="ident")
-        w_raw = [keep.tile([P, PACK, H], F32, name=f"w_raw{o}", tag=f"w_raw{o}") for o in range(PASSES)]
+        xs_tab = sb([P, T], U8, "xs_tab")
+        es_tab = sb([P, W], U8, "es_tab")
+        half_tab = sb([P, W], F32, "half_tab")
+        xw_tab = [sb([P, T], U32, f"xw_tab{o}") for o in range(PASSES)]
+        ew_tab = sb([P, W], U32, "ew_tab")
+        prior_sb = sb([P, V], F32, "prior_sb")
+        w_raw = [sb([P, PACK, H], F32, f"w_raw{o}") for o in range(PASSES)]
+        es_g = late.tile([P, U], U8, name="es_g", align_bytes=64, offset=768)
+        es_p = sb([P, U], U8, "es_p")
 
-        diff = keep.tile([P, P], F32, name="diff")
-        dist = keep.tile([P, P], F32, name="dist", align_bytes=64)
+        ident = sb([P, P], F32, "ident")
+        diff = sb([P, P], F32, "diff")
         nc.gpsimd.iota(diff[:], [[-1, P]], base=0, channel_multiplier=1, allow_small_or_imprecise_dtypes=True)
-        nc.scalar.activation(out=dist[:], in_=diff[:], func=ACT.Abs)
-        nc.scalar.activation(out=ident[:], in_=dist[:], func=ACT.Relu, scale=-1.0, bias=1.0)
-        es_g = keep.tile([P, U], U8, name="es_g", align_bytes=64)
-        es_p = keep.tile([P, U], U8, name="es_p", align_bytes=64)
+        nc.gpsimd.tensor_scalar(ident[:], diff[:], 0.0, 1.0, op0=ALU.is_equal, op1=ALU.mult)
+
+        zeros = sb([P, P], F32, "zeros")
+        nc.vector.memset(zeros[:], 0.0)
+        nc.scalar.copy(out=half_tab[:HALF_ROW, :P], in_=zeros[:HALF_ROW, :])
+
         nc.vector.memset(xs_tab[:].bitcast(I32), 0)
+        nc.vector.memset(half_tab[:HALF_ROW, P : W // 2].bitcast(I32), 0)
         nc.vector.memset(es_tab[:ES_ROW, :].bitcast(I32), 0)
-        nc.vector.memset(half_tab[:HALF_ROW, :].bitcast(I32), 0)
-        nc.vector.memset(es_p[:].bitcast(I32), 0)
+        nc.gpsimd.memset(half_tab[:HALF_ROW, W // 2 :].bitcast(I32), 0)
+        nc.gpsimd.memset(es_p[:].bitcast(I32), 0)
 
         def load_w(o):
-            rows = w1[o * 512 : (o + 1) * 512, :]
+            rows = w1[o * P * PACK : (o + 1) * P * PACK, :]
             nc.sync.dma_start(out=w_raw[o][:], in_=rows.rearrange("(p j) c -> p j c", j=PACK))
 
-        def load_x(o):
-            nc.sync.dma_start(
-                out=xw_tab[o][:].bitcast(I32), in_=x_words[o].rearrange("p n r -> p (n r)").bitcast(I32)
-            )
+        def load_words(tile, words):
+            nc.sync.dma_start(out=tile[:].bitcast(I32), in_=words.rearrange("p n r -> p (n r)").bitcast(I32))
 
         nc.sync.dma_start(pro_sb[:], pro)
         nc.sync.dma_start(out=es_tab[ES_ROW:, :].bitcast(I32), in_=e_scales[0].bitcast(I32))
+        nc.sync.dma_start(out=half_tab[HALF_ROW:, :], in_=half[0:1, :])
+        load_w(0)
         nc.sync.dma_start(offs_sb[:], offs)
-        nc.sync.dma_start(out=half_tab[HALF_ROW : HALF_ROW + 1, :], in_=half[0:1, :])
-        load_x(0)
         for q in range(4):
             nc.sync.dma_start(
                 out=xs_tab[32 * q : 32 * q + 8, :].bitcast(I32), in_=x_scales[:, 4 * q : 4 * q + 4, :].bitcast(I32)
             )
-        load_w(0)
+        load_words(xw_tab[0], x_words[0])
         load_w(1)
-        load_x(1)
-        nc.sync.dma_start(out=ew_tab[:].bitcast(I32), in_=e_words[0].rearrange("p n r -> p (n r)").bitcast(I32))
-        prior_in = late.tile([P, 768], F32, name="prior_in", align_bytes=64, offset=0)
-        nc.sync.dma_start(out=prior_in[:, :V], in_=prior)
-        nc.gpsimd.tensor_copy(prior_sb[:], prior_in[:, :V])
+        load_words(xw_tab[1], x_words[1])
+        load_words(ew_tab, e_words[0])
 
-        w_codes, w_scales, w_grouped = {}, {}, {}
+        nc.vector.tensor_copy(es_g[:].rearrange("p (s m) -> p m s", s=SIDES), es_tab[:].indirect(pro_sb[:]))
+        for q in range(4):
+            nc.sync.dma_start(
+                out=es_p[32 * q : 32 * q + 4, :].bitcast(I32),
+                in_=es_g[ES_ROW + 4 * q : ES_ROW + 4 * q + 4, :].bitcast(I32),
+            )
+        nc.sync.dma_start(out=prior_sb[:], in_=prior)
 
-        def group_w(o, pair, m0, m1, copy):
-            if (o, pair) not in w_grouped:
-                w_grouped[o, pair] = keep.tile(
-                    [P, 2 * H], BF16, name=f"w_grouped{o}_{pair}", tag=f"w_grouped{o}_{pair}", align_bytes=64
-                )
-            dst = w_grouped[o, pair][:].rearrange("p (t m j) -> p m j t", t=2, j=PACK)[:, m0:m1]
-            src = w_raw[o][:].rearrange("p j (m t) -> p m j t", t=PACK)[:, m0:m1, :, pair : pair + 2]
-            copy(out=dst, in_=src)
-
-        def quant_w(o, t0, t1, codes_tag):
-            n = t1 - t0
-            codes = keep.tile([P, n * P], U32, name=f"w_codes{o}_{t0}", tag=codes_tag, align_bytes=64)
-            scales = keep.tile([P, n * P], U8, name=f"w_scales{o}_{t0}", tag=f"w_scales{o}_{t0}", align_bytes=64)
-            nc.vector.quantize_mx(out=codes[:].bitcast(FP8X4), scales=scales[:], in_=w_grouped[o, t0][:])
-            for t in range(t0, t1):
-                w_codes[o, t] = codes[:, (t - t0) * P : (t - t0 + 1) * P]
-                w_scales[o, t] = scales[:, (t - t0) * P : (t - t0 + 1) * P]
-            return codes, scales
-
-        xs_g = keep.tile([P, S], U8, name="xs_g", align_bytes=64)
-        xw_g = {}
-
-        def xw_tile(o, g0, g1, tag):
-            tile = keep.tile([P, (g1 - g0) * P], U32, name=f"xw_g{o}_{g0}", tag=tag, align_bytes=64)
-            for g in range(g0, g1):
-                xw_g[o, g] = tile[:, (g - g0) * P : (g - g0 + 1) * P]
-            return tile
-
-        def gather_xw(o, g0, g1, dst):
-            nc.vector.tensor_copy(dst, xw_tab[o][:].indirect(offs_sb[:, g0 * 8 : g1 * 8]))
-
-        half_g = keep.tile([P, U], F32, name="half_g", tag="dist", align_bytes=64)
-        ew_g = {}
-
-        def gather_es():
-            nc.vector.tensor_copy(es_g[:].rearrange("p (h m) -> p m h", h=2), es_tab[:].indirect(pro_sb[:]))
-            for q in range(4):
-                nc.sync.dma_start(
-                    out=es_p[32 * q : 32 * q + 4, :].bitcast(I32),
-                    in_=es_g[ES_ROW + 4 * q : ES_ROW + 4 * q + 4, :].bitcast(I32),
-                )
-
-        def gather_ew(u, g):
-            ew_g[u] = g
-            nc.vector.tensor_copy(
-                g.rearrange("p (h m) -> p m h", h=2), ew_tab[:].indirect(pro_sb[:, u * 16 : (u + 1) * 16])
+        half_g = sb([P, U], F32, "half_g")
+        nc.scalar.activation(out=half_g[:], in_=half_tab[:].indirect(pro_sb[:]), func=ACT.Copy)
+        turned = bank([P, P + TURN_STEP * (NQ * SIDES - 1)], "turned", 4)
+        for i in reversed(range(NQ * SIDES)):
+            u, s = divmod(i, SIDES)
+            nc.tensor.transpose(
+                turned[:, i * TURN_STEP : i * TURN_STEP + P], half_g[:, u * QN + s : (u + 1) * QN : SIDES], ident[:]
             )
 
-        def negate_half(banks):
-            nb = keep.tile([P, 2, NQ], F32, name="nbias", tag="w_raw1")
-            for h in range(2):
-                nc.scalar.activation(out=nb[:, h, :], in_=banks[h][:, :, HALF_ROW], func=ACT.Copy, scale=-1.0)
-            return nb
+        w_bf_first = sb([P, 2, 2 * H], BF16, "w_bf_first", tag="half_tab")
+        w_bf = {(0, a): w_bf_first[:, a // 2, :] for a in (0, 2)}
+        for a in (0, 2):
+            w_bf[1, a] = sb([P, 2 * H], BF16, f"w_bf1_{a}")[:]
+        w_codes, w_scales = {}, {}
 
-        def turn_half():
-            banks = []
-            for h in range(2):
-                bank = psum.tile([P, NQ, P], F32, name="turn", tag=f"bank{4 + h}")
-                for u in range(NQ):
-                    nc.tensor.transpose(bank[:, u, :], half_g[:, u * QN + h : (u + 1) * QN : 2], ident[:])
-                banks.append(bank)
-            return banks
+        def cast_w(o, a, m0, m1, copy):
+            dst = w_bf[o, a].rearrange("p (t m j) -> p m j t", t=2, j=PACK)[:, m0:m1]
+            src = w_raw[o][:].rearrange("p j (m t) -> p m j t", t=PACK)[:, m0:m1, :, a : a + 2]
+            copy(out=dst, in_=src)
 
-        h_bf = [keep.tile([P, HALF, PACK], BF16, name=f"h_bf{i}", tag=f"h_bf{i}", align_bytes=64) for i in range(2)]
-        h_codes = late.tile([P, S], U32, name="h_codes", align_bytes=64, offset=0)
-        h_scales = keep.tile([P, S], U8, name="h_scales", align_bytes=64)
+        def quant_w(o, a):
+            codes = sb([P, 2 * P], U32, f"w_codes{o}_{a}")
+            scales = sb([P, 2 * P], U8, f"w_scales{o}_{a}")
+            nc.vector.quantize_mx(out=codes[:].bitcast(FP8X4), scales=scales[:], in_=w_bf[o, a])
+            for t in range(2):
+                w_codes[o, a + t] = codes[:, t * P : (t + 1) * P]
+                w_scales[o, a + t] = scales[:, t * P : (t + 1) * P]
 
-        h_bank = [psum.tile([P, PACK, P], F32, name="h_bank", tag=f"bank{g}") for g in range(4)]
+        xs_g = sb([P, S], U8, "xs_g")
+        xw_g = {}
 
-        def first_product(o, g):
-            order = (0, 1, 2, 3)
-            for t in order:
+        def gather_x(o, g0, g1):
+            tile = sb([P, (g1 - g0) * P], U32, f"xw_g{o}_{g0}")
+            nc.vector.tensor_copy(tile[:], xw_tab[o][:].indirect(offs_sb[:, g0 * P // 16 : g1 * P // 16]))
+            for g in range(g0, g1):
+                xw_g[o, g] = tile[:, (g - g0) * P : (g - g0 + 1) * P]
+
+        h_bank = [bank([P, PACK, P], "h_bank", g) for g in range(BLOCKS)]
+        h_bf = [sb([P, HALF, PACK], BF16, f"h_bf{i}") for i in range(2)]
+        h_codes = sb([P, S], U32, "h_codes")
+        h_scales = late.tile([P, S], U8, name="h_scales", align_bytes=64, offset=1024)
+
+        def first_product(o, g, ts):
+            for t in ts:
                 nc.tensor.matmul_mx(
                     out=h_bank[g][:, t, :],
                     lhsT=w_codes[o, t].bitcast(FP8X4),
                     lhsT_scale=w_scales[o, t],
                     rhs=xw_g[o, g].bitcast(FP8X4),
                     rhs_scale=xs_g[4 * o : P, g * P : (g + 1) * P],
-                    start=(o == 0 and t == order[0]),
-                    stop=(o == PASSES - 1 and t == order[-1]),
+                    start=(o == 0 and t == 0),
+                    stop=(o == PASSES - 1 and t == PACK - 1),
                 )
 
         def copy_h(g):
             c0 = (g % 2) * P
             nc.scalar.copy(out=h_bf[g // 2][:, c0 : c0 + P, :], in_=h_bank[g][:].rearrange("p t n -> p n t"))
 
-        def quant_h(i):
-            cols = slice(i * HALF, (i + 1) * HALF)
+        def quant_h(t0, t1):
+            c0 = t0 % HALF
             nc.vector.quantize_mx(
-                out=h_codes[:, cols].bitcast(FP8X4),
-                scales=h_scales[:, cols],
-                in_=h_bf[i][:].rearrange("p n t -> p (n t)"),
+                out=h_codes[:, t0:t1].bitcast(FP8X4),
+                scales=h_scales[:, t0:t1],
+                in_=h_bf[t0 // HALF][:, c0 : c0 + t1 - t0, :].rearrange("p n t -> p (n t)"),
             )
 
-        sums = keep.tile([P, 4, V], F32, name="sums")
-        ee = [keep.tile([P, 2, S], F32, name=f"ee{u}", tag=f"ee{u}") for u in range(NQ)]
+        cast_w(0, 0, 0, P, nc.scalar.copy)
+        cast_w(0, 2, 0, P, nc.scalar.copy)
+        nc.vector.tensor_copy(xs_g[:], xs_tab[:].indirect(offs_sb[:]))
+        quant_w(0, 0)
+        gather_x(0, 0, 2)
+        gather_x(0, 2, 4)
+        quant_w(0, 2)
+        for g in range(BLOCKS):
+            first_product(0, g, range(PACK))
+        nbias = sb([P, NQ * SIDES], F32, "nbias", tag="w_raw0")
+        nc.scalar.activation(out=nbias[:], in_=turned[:, HALF_ROW::TURN_STEP], func=ACT.Copy, scale=-1.0)
 
-        def second_product(u, t0, t1, slots):
+        cast_w(1, 0, 0, P, nc.vector.tensor_copy)
+        cast_w(1, 2, 0, P, nc.scalar.copy)
+        quant_w(1, 0)
+        gather_x(1, 0, 1)
+        quant_w(1, 2)
+        gather_x(1, 1, 2)
+        gather_x(1, 2, 3)
+        gather_x(1, 3, 4)
+        for g in range(BLOCKS):
+            first_product(1, g, range(PACK))
+            copy_h(g)
+
+        ew_last = sb([P, 2, QN], U32, "ew_last", tag="h_bf1")
+        ew_g = [
+            sb([P, QN], U32, "ew_g0")[:],
+            late.tile([P, QN], U32, name="ew_g1", align_bytes=64, offset=0)[:],
+            ew_last[:, 0, :],
+            ew_last[:, 1, :],
+        ]
+
+        def gather_e(u):
+            nc.vector.tensor_copy(
+                ew_g[u].rearrange("p (s m) -> p m s", s=SIDES),
+                ew_tab[:].indirect(pro_sb[:, u * QN // 16 : (u + 1) * QN // 16]),
+            )
+
+        ee = [sb([P, SIDES, S], F32, f"ee{u}") for u in range(NQ)]
+
+        def second_product(u, t0, t1, slots, step=None):
             n = t1 - t0
             if len(slots) == 1:
-                bank = psum.tile([P, 2, n], F32, name="y_bank", tag=f"bank{slots[0]}")
-                y = [bank[:, h, :] for h in range(2)]
+                both = bank([P, SIDES, n], "y_bank", slots[0])
+                y = [both[:, s, :] for s in range(SIDES)]
             else:
-                y = [psum.tile([P, n], F32, name="y_bank", tag=f"bank{slots[h]}")[:] for h in range(2)]
-            for h in range(2):
-                nc.tensor.matmul_mx(
-                    out=y[h],
-                    lhsT=ew_g[u][:, h * P : (h + 1) * P].bitcast(FP8X4),
-                    lhsT_scale=es_p[:, h * U // 2 + u * P : h * U // 2 + (u + 1) * P],
-                    rhs=h_codes[:, t0:t1].bitcast(FP8X4),
-                    rhs_scale=h_scales[:, t0:t1],
-                    start=True,
-                    stop=True,
-                )
-            for h in range(2):
-                nc.scalar.activation(out=ee[u][:, h, t0:t1], in_=y[h], func=ACT.Exp, bias=nbias[:, h, u : u + 1])
+                y = [bank([P, n], "y_bank", slot)[:] for slot in slots]
+            step = step or n
+            for c in range(t0, t1, step):
+                for s in range(SIDES):
+                    nc.tensor.matmul_mx(
+                        out=y[s][:, c - t0 : c - t0 + step],
+                        lhsT=ew_g[u][:, s * P : (s + 1) * P].bitcast(FP8X4),
+                        lhsT_scale=es_p[:, s * U // SIDES + u * P : s * U // SIDES + (u + 1) * P],
+                        rhs=h_codes[:, c : c + step].bitcast(FP8X4),
+                        rhs_scale=h_scales[:, c : c + step],
+                        start=True,
+                        stop=True,
+                    )
+            for s in range(SIDES):
+                i = u * SIDES + s
+                nc.scalar.activation(out=ee[u][:, s, t0:t1], in_=y[s], func=ACT.Exp, bias=nbias[:, i : i + 1])
 
-        def sum_up(u0, u1, i, slot):
-            n = u1 - u0
-            bank = psum.tile([P, 2, n, P], F32, name="acc", tag=f"bank{slot}")
-            for u in range(u0, u1):
-                for g in range(2):
-                    t0 = i * HALF + g * P
-                    for h in range(2):
-                        nc.tensor.matmul(
-                            out=bank[:, g, u - u0, :],
-                            lhsT=ee[u][:, h, t0 : t0 + P],
-                            rhs=ident[:],
-                            start=(h == 0),
-                            stop=(h == 1),
-                            is_transpose=True,
-                        )
+        gather_e(0)
+        quant_h(0, P)
+        quant_h(P, HALF)
+        gather_e(1)
+        quant_h(HALF, S)
+        gather_e(2)
+        gather_e(3)
+        second_product(0, 0, HALF, (5, 6), step=P)
+        second_product(1, 0, HALF, (7,))
+        second_product(0, HALF, S, (4,))
+        second_product(1, HALF, S, (0,))
+        second_product(2, 0, S, (1, 2))
+        second_product(3, 0, S, (3, 5))
+
+        sums = sb([P, BLOCKS, V], F32, "sums")
+        CQ = V // NQ
+
+        def sum_up(pairs, slot, dst):
+            acc = bank([P, len(pairs), P], "acc", slot)
+            for s in range(SIDES):
+                for i, (g, u) in enumerate(pairs):
+                    nc.tensor.matmul(
+                        out=acc[:, i, :],
+                        lhsT=ee[u][:, s, g * P : (g + 1) * P],
+                        rhs=ident[:],
+                        start=(s == 0 and i == 0),
+                        stop=(s == SIDES - 1 and i == len(pairs) - 1),
+                        is_transpose=True,
+                    )
             nc.vector.tensor_reduce(
-                out=sums[:, 2 * i : 2 * i + 2, 32 * u0 : 32 * u1],
-                in_=bank[:].rearrange("p g u (v d) -> p g (u v) d", d=4),
+                out=dst,
+                in_=acc[:].rearrange("p (g u) (v d) -> p g (u v) d", g=dst.shape[1], d=D // SIDES),
                 axis=AX.X,
                 op=ALU.add,
             )
 
-        def gather_half(i):
-            n = U // 2
-            nc.scalar.activation(
-                out=half_g[:, i * n : (i + 1) * n],
-                in_=half_tab[:].indirect(pro_sb[:, i * n // 16 : (i + 1) * n // 16]),
-                func=ACT.Copy,
-            )
+        for i in range(2):
+            sum_up([(g, u) for g in (2 * i, 2 * i + 1) for u in (0, 1)], 6 + i, sums[:, 2 * i : 2 * i + 2, : 2 * CQ])
+        for u, slot in ((2, 4), (3, 0)):
+            sum_up([(g, u) for g in range(BLOCKS)], slot, sums[:, :, u * CQ : (u + 1) * CQ])
 
-        gather_es()
-        gather_xw(0, 0, 4, xw_tile(0, 0, 4, "xw_g0")[:])
-        nc.vector.tensor_copy(xs_g[:], xs_tab[:].indirect(offs_sb[:]))
-        gather_half(0)
-        gather_half(1)
-        group_w(0, 0, 0, P, nc.scalar.copy)
-        group_w(0, 2, 0, P, nc.scalar.copy)
-        quant_w(0, 0, 2, "w_codes0_0")
-        quant_w(0, 2, 4, "w_codes0_2")
-        group_w(1, 0, 0, P, nc.scalar.copy)
-        group_w(1, 2, P // 2, P, nc.vector.tensor_copy)
-        group_w(1, 2, 0, P // 2, nc.scalar.copy)
-        quant_w(1, 0, 2, "w_codes1_0")
-        gather_xw(1, 0, 2, xw_tile(1, 0, 2, "xw_g1_0")[:])
-        quant_w(1, 2, 4, "w_codes1_2")
-        turned = turn_half()
-        gather_xw(1, 2, 4, xw_tile(1, 2, 4, "w_grouped1_2")[:])
-        for g in range(4):
-            first_product(0, g)
-        nbias = negate_half(turned)
-        for g in range(4):
-            first_product(1, g)
-            copy_h(g)
-        gather_ew(0, keep.tile([P, QN], U32, name="ew_g0", align_bytes=64)[:])
-        quant_h(0)
-        gather_ew(1, late.tile([P, QN], U32, name="ew_g1", align_bytes=64, offset=2048)[:])
-        quant_h(1)
-        ew_last = keep.tile([P, 2 * QN], U32, name="ew_last", tag="h_bf1", align_bytes=64)
-        gather_ew(2, ew_last[:, :QN])
-        gather_ew(3, ew_last[:, QN:])
-        second_product(0, 0, HALF, (4, 5))
-        second_product(1, 0, HALF, (6,))
-        second_product(0, HALF, S, (7, 0))
-        second_product(1, HALF, S, (1,))
-        second_product(2, 0, S, (2, 3))
-        second_product(3, 0, HALF, (4,))
-        second_product(3, HALF, S, (5,))
-        sum_up(0, 2, 0, 6)
-        sum_up(0, 2, 1, 1)
-        sum_up(2, 4, 0, 7)
-        sum_up(2, 3, 1, 0)
-        sum_up(3, 4, 1, 2)
-
-        res_first = keep.tile([P, 2, V], F32, name="res_first", tag="ee3")
-        res_second = keep.tile([P, 2, V], F32, name="res_second")
-        for g in range(4):
+        for g in range(BLOCKS):
             logs = ring.tile([P, V], F32, name="logs")
             nc.scalar.activation(out=logs[:], in_=sums[:, g, :], func=ACT.Ln)
-            res = (res_first if g < 2 else res_second)[:, g % 2, :]
-            nc.vector.tensor_tensor(out=res, in0=logs[:], in1=prior_sb[:], op=ALU.add)
-            nc.sync.dma_start(out=out[g * P : (g + 1) * P, :], in_=res)
+            res = ring.tile([P, V], F32, name="res")
+            nc.vector.tensor_tensor(out=res[:], in0=logs[:], in1=prior_sb[:], op=ALU.add)
+            nc.sync.dma_start(out=out[g * P : (g + 1) * P, :], in_=res[:])

from contextlib import ExitStack

import concourse.mybir as mybir

K, T, S, H, D, V, W, U = 1024, 1024, 512, 512, 8, 128, 2048, 1024
FLOPS = 2 * K * H * S + 2 * H * S * U

F32 = mybir.dt.float32
BF16 = mybir.dt.bfloat16
I32 = mybir.dt.int32
U32 = mybir.dt.uint32
U16 = mybir.dt.uint16
U8 = mybir.dt.uint8
FP8X4 = mybir.dt.float8_e4m3fn_x4
ACT = mybir.ActivationFunctionType
ALU = mybir.AluOpType
AX = mybir.AxisListType

P = 128
PACK = 4
PASSES = K // (P * PACK)
BLOCKS = S // P
HALF = S // 2
SIDES = 2
NQ = 4
QN = U // NQ
ES_ROW = P - 16
HALF_ROW = P - 1
TURN_STEP = 16


def tile_picked_yparz_log_p_kernel(
    tc, x_words, x_scales, w1, e_words, e_scales, half, prior, offs, pro, out
):
    nc = tc.nc
    with ExitStack() as ctx:
        lists = ctx.enter_context(tc.tile_pool(name="lists", bufs=1))
        keep = ctx.enter_context(tc.tile_pool(name="keep", bufs=1))
        ring = ctx.enter_context(tc.tile_pool(name="ring", bufs=4))
        late = ctx.enter_context(tc.tile_pool(name="late", bufs=1))
        psum = ctx.enter_context(tc.psum_pool(name="psum", bufs=1))

        def sb(shape, dtype, name, tag=None):
            return keep.tile(shape, dtype, name=name, tag=tag or name, align_bytes=64)

        def bank(shape, name, slot):
            return psum.tile(shape, F32, name=name, tag=f"bank{slot}")

        offs_sb = lists.tile([P, S // 16], U16, name="offs_sb")
        pro_sb = lists.tile([P, U // 16], U16, name="pro_sb")

        xs_tab = sb([P, T], U8, "xs_tab")
        es_tab = sb([P, W], U8, "es_tab")
        half_tab = sb([P, W], F32, "half_tab")
        xw_tab = [sb([P, T], U32, f"xw_tab{o}") for o in range(PASSES)]
        ew_tab = sb([P, W], U32, "ew_tab")
        prior_sb = sb([P, V], F32, "prior_sb")
        w_raw = [sb([P, PACK, H], F32, f"w_raw{o}") for o in range(PASSES)]
        es_g = late.tile([P, U], U8, name="es_g", align_bytes=64, offset=768)
        es_p = sb([P, U], U8, "es_p")

        ident = sb([P, P], F32, "ident")
        diff = sb([P, P], F32, "diff")
        nc.gpsimd.iota(diff[:], [[-1, P]], base=0, channel_multiplier=1, allow_small_or_imprecise_dtypes=True)
        nc.gpsimd.tensor_scalar(ident[:], diff[:], 0.0, 1.0, op0=ALU.is_equal, op1=ALU.mult)

        zeros = sb([P, P], F32, "zeros")
        nc.vector.memset(zeros[:], 0.0)
        nc.scalar.copy(out=half_tab[:HALF_ROW, :P], in_=zeros[:HALF_ROW, :])

        nc.vector.memset(xs_tab[:].bitcast(I32), 0)
        nc.vector.memset(half_tab[:HALF_ROW, P : W // 2].bitcast(I32), 0)
        nc.vector.memset(es_tab[:ES_ROW, :].bitcast(I32), 0)
        nc.gpsimd.memset(half_tab[:HALF_ROW, W // 2 :].bitcast(I32), 0)
        nc.gpsimd.memset(es_p[:].bitcast(I32), 0)

        def load_w(o):
            rows = w1[o * P * PACK : (o + 1) * P * PACK, :]
            nc.sync.dma_start(out=w_raw[o][:], in_=rows.rearrange("(p j) c -> p j c", j=PACK))

        def load_words(tile, words):
            nc.sync.dma_start(out=tile[:].bitcast(I32), in_=words.rearrange("p n r -> p (n r)").bitcast(I32))

        nc.sync.dma_start(pro_sb[:], pro)
        nc.sync.dma_start(out=es_tab[ES_ROW:, :].bitcast(I32), in_=e_scales[0].bitcast(I32))
        nc.sync.dma_start(out=half_tab[HALF_ROW:, :], in_=half[0:1, :])
        load_w(0)
        nc.sync.dma_start(offs_sb[:], offs)
        for q in range(4):
            nc.sync.dma_start(
                out=xs_tab[32 * q : 32 * q + 8, :].bitcast(I32), in_=x_scales[:, 4 * q : 4 * q + 4, :].bitcast(I32)
            )
        load_words(xw_tab[0], x_words[0])
        load_w(1)
        load_words(xw_tab[1], x_words[1])
        load_words(ew_tab, e_words[0])

        nc.vector.tensor_copy(es_g[:].rearrange("p (s m) -> p m s", s=SIDES), es_tab[:].indirect(pro_sb[:]))
        for q in range(4):
            nc.sync.dma_start(
                out=es_p[32 * q : 32 * q + 4, :].bitcast(I32),
                in_=es_g[ES_ROW + 4 * q : ES_ROW + 4 * q + 4, :].bitcast(I32),
            )
        nc.sync.dma_start(out=prior_sb[:], in_=prior)

        half_g = sb([P, U], F32, "half_g")
        nc.scalar.activation(out=half_g[:], in_=half_tab[:].indirect(pro_sb[:]), func=ACT.Copy)
        turned = bank([P, P + TURN_STEP * (NQ * SIDES - 1)], "turned", 4)
        for i in reversed(range(NQ * SIDES)):
            u, s = divmod(i, SIDES)
            nc.tensor.transpose(
                turned[:, i * TURN_STEP : i * TURN_STEP + P], half_g[:, u * QN + s : (u + 1) * QN : SIDES], ident[:]
            )

        w_bf_first = sb([P, 2, 2 * H], BF16, "w_bf_first", tag="half_tab")
        w_bf = {(0, a): w_bf_first[:, a // 2, :] for a in (0, 2)}
        for a in (0, 2):
            w_bf[1, a] = sb([P, 2 * H], BF16, f"w_bf1_{a}")[:]
        w_codes, w_scales = {}, {}

        def cast_w(o, a, m0, m1, copy):
            dst = w_bf[o, a].rearrange("p (t m j) -> p m j t", t=2, j=PACK)[:, m0:m1]
            src = w_raw[o][:].rearrange("p j (m t) -> p m j t", t=PACK)[:, m0:m1, :, a : a + 2]
            copy(out=dst, in_=src)

        def quant_w(o, a):
            codes = sb([P, 2 * P], U32, f"w_codes{o}_{a}")
            scales = sb([P, 2 * P], U8, f"w_scales{o}_{a}")
            nc.vector.quantize_mx(out=codes[:].bitcast(FP8X4), scales=scales[:], in_=w_bf[o, a])
            for t in range(2):
                w_codes[o, a + t] = codes[:, t * P : (t + 1) * P]
                w_scales[o, a + t] = scales[:, t * P : (t + 1) * P]

        xs_g = sb([P, S], U8, "xs_g")
        xw_g = {}

        def gather_x(o, g0, g1):
            tile = sb([P, (g1 - g0) * P], U32, f"xw_g{o}_{g0}")
            nc.vector.tensor_copy(tile[:], xw_tab[o][:].indirect(offs_sb[:, g0 * P // 16 : g1 * P // 16]))
            for g in range(g0, g1):
                xw_g[o, g] = tile[:, (g - g0) * P : (g - g0 + 1) * P]

        h_bank = [bank([P, PACK, P], "h_bank", g) for g in range(BLOCKS)]
        h_bf = [sb([P, HALF, PACK], BF16, f"h_bf{i}") for i in range(2)]
        h_codes = sb([P, S], U32, "h_codes")
        h_scales = late.tile([P, S], U8, name="h_scales", align_bytes=64, offset=1024)

        def first_product(o, g, ts):
            for t in ts:
                nc.tensor.matmul_mx(
                    out=h_bank[g][:, t, :],
                    lhsT=w_codes[o, t].bitcast(FP8X4),
                    lhsT_scale=w_scales[o, t],
                    rhs=xw_g[o, g].bitcast(FP8X4),
                    rhs_scale=xs_g[4 * o : P, g * P : (g + 1) * P],
                    start=(o == 0 and t == 0),
                    stop=(o == PASSES - 1 and t == PACK - 1),
                )

        def copy_h(g):
            c0 = (g % 2) * P
            nc.scalar.copy(out=h_bf[g // 2][:, c0 : c0 + P, :], in_=h_bank[g][:].rearrange("p t n -> p n t"))

        def quant_h(t0, t1):
            c0 = t0 % HALF
            nc.vector.quantize_mx(
                out=h_codes[:, t0:t1].bitcast(FP8X4),
                scales=h_scales[:, t0:t1],
                in_=h_bf[t0 // HALF][:, c0 : c0 + t1 - t0, :].rearrange("p n t -> p (n t)"),
            )

        cast_w(0, 0, 0, P, nc.scalar.copy)
        cast_w(0, 2, 0, P, nc.scalar.copy)
        nc.vector.tensor_copy(xs_g[:], xs_tab[:].indirect(offs_sb[:]))
        quant_w(0, 0)
        gather_x(0, 0, 2)
        gather_x(0, 2, 4)
        quant_w(0, 2)
        for g in range(BLOCKS):
            first_product(0, g, range(PACK))
        nbias = sb([P, NQ * SIDES], F32, "nbias", tag="w_raw0")
        nc.scalar.activation(out=nbias[:], in_=turned[:, HALF_ROW::TURN_STEP], func=ACT.Copy, scale=-1.0)

        cast_w(1, 0, 0, P, nc.vector.tensor_copy)
        cast_w(1, 2, 0, P, nc.scalar.copy)
        quant_w(1, 0)
        gather_x(1, 0, 1)
        quant_w(1, 2)
        gather_x(1, 1, 2)
        gather_x(1, 2, 3)
        gather_x(1, 3, 4)
        for g in range(BLOCKS):
            first_product(1, g, range(PACK))
            copy_h(g)

        ew_last = sb([P, 2, QN], U32, "ew_last", tag="h_bf1")
        ew_g = [
            sb([P, QN], U32, "ew_g0")[:],
            late.tile([P, QN], U32, name="ew_g1", align_bytes=64, offset=0)[:],
            ew_last[:, 0, :],
            ew_last[:, 1, :],
        ]

        def gather_e(u):
            nc.vector.tensor_copy(
                ew_g[u].rearrange("p (s m) -> p m s", s=SIDES),
                ew_tab[:].indirect(pro_sb[:, u * QN // 16 : (u + 1) * QN // 16]),
            )

        ee = [sb([P, SIDES, S], F32, f"ee{u}") for u in range(NQ)]

        def second_product(u, t0, t1, slots, step=None):
            n = t1 - t0
            if len(slots) == 1:
                both = bank([P, SIDES, n], "y_bank", slots[0])
                y = [both[:, s, :] for s in range(SIDES)]
            else:
                y = [bank([P, n], "y_bank", slot)[:] for slot in slots]
            step = step or n
            for c in range(t0, t1, step):
                for s in range(SIDES):
                    nc.tensor.matmul_mx(
                        out=y[s][:, c - t0 : c - t0 + step],
                        lhsT=ew_g[u][:, s * P : (s + 1) * P].bitcast(FP8X4),
                        lhsT_scale=es_p[:, s * U // SIDES + u * P : s * U // SIDES + (u + 1) * P],
                        rhs=h_codes[:, c : c + step].bitcast(FP8X4),
                        rhs_scale=h_scales[:, c : c + step],
                        start=True,
                        stop=True,
                    )
            for s in range(SIDES):
                i = u * SIDES + s
                nc.scalar.activation(out=ee[u][:, s, t0:t1], in_=y[s], func=ACT.Exp, bias=nbias[:, i : i + 1])

        gather_e(0)
        quant_h(0, P)
        quant_h(P, HALF)
        gather_e(1)
        quant_h(HALF, S)
        gather_e(2)
        gather_e(3)
        second_product(0, 0, HALF, (5, 6), step=P)
        second_product(1, 0, HALF, (7,))
        second_product(0, HALF, S, (4,))
        second_product(1, HALF, S, (0,))
        second_product(2, 0, S, (1, 2))
        second_product(3, 0, S, (3, 5))

        sums = sb([P, BLOCKS, V], F32, "sums")
        CQ = V // NQ

        def sum_up(pairs, slot, dst):
            acc = bank([P, len(pairs), P], "acc", slot)
            for s in range(SIDES):
                for i, (g, u) in enumerate(pairs):
                    nc.tensor.matmul(
                        out=acc[:, i, :],
                        lhsT=ee[u][:, s, g * P : (g + 1) * P],
                        rhs=ident[:],
                        start=(s == 0 and i == 0),
                        stop=(s == SIDES - 1 and i == len(pairs) - 1),
                        is_transpose=True,
                    )
            nc.vector.tensor_reduce(
                out=dst,
                in_=acc[:].rearrange("p (g u) (v d) -> p g (u v) d", g=dst.shape[1], d=D // SIDES),
                axis=AX.X,
                op=ALU.add,
            )

        for i in range(2):
            sum_up([(g, u) for g in (2 * i, 2 * i + 1) for u in (0, 1)], 6 + i, sums[:, 2 * i : 2 * i + 2, : 2 * CQ])
        for u, slot in ((2, 4), (3, 0)):
            sum_up([(g, u) for g in range(BLOCKS)], slot, sums[:, :, u * CQ : (u + 1) * CQ])

        for g in range(BLOCKS):
            logs = ring.tile([P, V], F32, name="logs")
            nc.scalar.activation(out=logs[:], in_=sums[:, g, :], func=ACT.Ln)
            res = ring.tile([P, V], F32, name="res")
            nc.vector.tensor_tensor(out=res[:], in0=logs[:], in1=prior_sb[:], op=ALU.add)
            nc.sync.dma_start(out=out[g * P : (g + 1) * P, :], in_=res[:])
